import numpy as np
import ml_dtypes


def mxq(x, axis, fmt="e4m3"):
    dtype, down = {"e4m3": (ml_dtypes.float8_e4m3fn, 7), "e5m2": (ml_dtypes.float8_e5m2, 14)}[fmt]
    v = np.moveaxis(np.asarray(x, np.float32).astype(ml_dtypes.bfloat16).astype(np.float64), axis, -1)
    blocks = v.reshape(v.shape[:-1] + (-1, 32))
    amax = np.abs(blocks).max(-1, keepdims=True)
    byte = np.maximum(np.where(amax > 0, np.frexp(amax)[1] - 1 + 127, 0) - down, 1)
    scale = np.exp2(byte - 127.0)
    codes = (blocks / scale).astype(np.float32).astype(dtype).astype(np.float64)
    return np.moveaxis((codes * scale).reshape(v.shape), -1, axis)


WIDE = False


def mx_kscale(k):
    if not WIDE:
        return np.ones(k)
    levels = np.array([10, -10, 5, -5, 0])
    if k % 512:
        return np.exp2(np.random.permutation(np.resize(levels, k // 32))).repeat(32)
    a = np.empty((k // 512, 16))
    for p in range(k // 512):
        a[p, :8] = np.random.permutation(np.resize(levels, 8))
        for g in range(8):
            far = levels[np.abs(levels - a[p, g]) >= 10]
            a[p, g + 8] = far[np.random.randint(len(far))]
    return np.exp2(a.ravel()).repeat(32)


BF16 = ml_dtypes.bfloat16


def bf(x):
    return np.asarray(x, np.float32).astype(BF16)


def f64(x):
    return np.asarray(x).astype(np.float64)


N, M, D, E = 2048, 1024, 512, 512
RADIUS = 16.0
BETA = 2.0


def softmax(a):
    e = np.exp(a - a.max(-1, keepdims=True))
    return e / e.sum(-1, keepdims=True)


def value_time(v, g):
    gv = g[:, None] * v
    return np.sqrt(RADIUS**2 + np.sum(gv * gv, axis=-1))


def draw0():
    s, t = mx_kscale(D), mx_kscale(M)
    c = 0.95 / D**0.25
    return {"q": bf(np.random.standard_normal((N, D)) * c * s),
            "qt": bf(4.6 + 0.15 * np.random.standard_normal(N)),
            "k": bf(np.random.standard_normal((M, D)) * c / s),
            "kt": bf(4.6 + 0.15 * np.random.standard_normal(M)),
            "v": bf(np.random.standard_normal((M, E)) / t[:, None]),
            "g": bf(np.random.standard_normal(M) * t)}


def core(q, qt, k, kt, v, g):
    qt, kt, v, g = f64(qt), f64(kt), f64(v), f64(g)
    l = (mxq(f64(q), 1, "e4m3") @ mxq(f64(k), 1, "e4m3").T) - qt[:, None] * kt[None, :]
    p = softmax(BETA * l)
    pg = p * g[None, :]
    us = mxq(pg, 1, "e4m3") @ mxq(v, 0, "e4m3")
    vt = value_time(v, g)
    ut = np.sum(p * vt[None, :], axis=-1)
    root = np.sqrt(ut * ut - np.sum(us * us, axis=-1))
    return RADIUS * us / root[:, None]


def e4m3fn_bytes(y):
    return np.clip(np.asarray(y, np.float64), -448.0, 448.0).astype(np.float32).astype(ml_dtypes.float8_e4m3fn).view(np.uint8)


def e4m3fn_values(b):
    return np.asarray(b, np.uint8).view(ml_dtypes.float8_e4m3fn).astype(np.float64)


def setup_inputs():
    d = draw0()
    x0 = np.asarray(d['q']).astype(np.float64)
    s = (np.max(np.abs(x0), axis=(0,), keepdims=True) / 448.0).astype(np.float32)
    out = {}
    for k, v in d.items():
        if k == 'q':
            out['q_bytes'] = e4m3fn_bytes(x0 / s.astype(np.float64))
            out['q_scale'] = s
        else:
            out[k] = v
    return out


def reference(q_bytes, q_scale, qt, k, kt, v, g):
    return core(e4m3fn_values(q_bytes) * q_scale.astype(np.float64), qt, k, kt, v, g)

@@ -1,0 +1,431 @@
+from contextlib import ExitStack
+
+import concourse.mybir as mybir
+from concourse.masks import make_identity
+
+N, M, D, E = 2048, 1024, 512, 512
+FLOPS = 2 * N * M * D + 2 * N * M * E
+
+F32 = mybir.dt.float32
+BF16 = mybir.dt.bfloat16
+U32 = mybir.dt.uint32
+U8 = mybir.dt.uint8
+FP8 = mybir.dt.float8_e4m3fn
+FP8X4 = mybir.dt.float8_e4m3fn_x4
+ALU = mybir.AluOpType
+ACT = mybir.ActivationFunctionType
+AX = mybir.AxisListType
+
+P = 128
+T = N // P
+UT_ON_VECTOR = (15,)
+C = M // 512
+
+
+def tile_lorentzcentroidaggregation_kernel(tc, q_bytes, q_scale, qt, k, kt, v, g, out):
+    nc = tc.nc
+    with ExitStack() as ctx:
+        keep = ctx.enter_context(tc.tile_pool(name="keep", bufs=1))
+        work = ctx.enter_context(tc.tile_pool(name="work", bufs=2))
+        psum = ctx.enter_context(tc.psum_pool(name="psum", bufs=1))
+        ctx.enter_context(tc.manual_schedule())
+
+        q_raw = keep.tile([P, T, D], U8, name="q_raw")
+        k_raw = keep.tile([P, C, 4, D], BF16, name="k_raw")
+        v_raw = keep.tile([P, C, 4, E], BF16, name="v_raw")
+        qs = keep.tile([P, D], F32, name="qs")
+        qt_b = keep.tile([P, T], BF16, name="qt_b")
+        kt_b = keep.tile([P, C, 4], BF16, name="kt_b")
+        g_b = keep.tile([P, C, 4], BF16, name="g_b")
+
+        q_view = q_bytes.rearrange("(p i) d -> p i d", i=T)
+        k_view = k.rearrange("(c p j) d -> p c j d", c=C, j=4)
+        v_view = v.rearrange("(c p j) e -> p c j e", c=C, j=4)
+        nc.scalar.dma_start(out=kt_b[:], in_=kt.rearrange("(c p j) -> p c j", c=C, j=4))
+        nc.scalar.dma_start(out=g_b[:], in_=g.rearrange("(c p j) -> p c j", c=C, j=4))
+        nc.scalar.dma_start(out=qt_b[:], in_=qt.rearrange("(p i) -> p i", i=T))
+        nc.sync.dma_start(out=k_raw[:, 0, 0:2, :], in_=k_view[:, 0, 0:2, :])
+        nc.sync.dma_start(out=qs[:], in_=q_scale.rearrange("o d -> (o d)").partition_broadcast(P))
+        nc.sync.dma_start(out=q_raw[:, 0:2, :], in_=q_view[:, 0:2, :])
+        nc.sync.dma_start(out=k_raw[:, 0, 2:4, :], in_=k_view[:, 0, 2:4, :])
+        nc.sync.dma_start(out=k_raw[:, 1, :, :], in_=k_view[:, 1, :, :])
+        nc.sync.dma_start(out=q_raw[:, 2:8, :], in_=q_view[:, 2:8, :])
+        nc.sync.dma_start(out=v_raw[:, 0, :, :], in_=v_view[:, 0, :, :])
+        nc.sync.dma_start(out=v_raw[:, 1, :, :], in_=v_view[:, 1, :, :])
+        nc.sync.dma_start(out=q_raw[:, 8:16, :], in_=q_view[:, 8:16, :])
+
+        ident = keep.tile([P, P], F32, name="ident")
+        make_identity(nc, ident[:])
+        half = keep.tile([P, 8], F32, name="half")
+        nhalf = keep.tile([P, 1], F32, name="nhalf")
+        nc.gpsimd.memset(half[:], 0.5)
+        nc.gpsimd.memset(nhalf[:], -0.5)
+        warm = keep.tile([P, 1], F32, name="warm")
+        nc.vector.memset(warm[:], 0.0)
+        warm_o = keep.tile([P, 1], F32, name="warm_o")
+        nc.scalar.activation(warm_o[:], warm[:], ACT.Exp)
+
+        spread = keep.tile([P, 2, P, 2], BF16, name="spread")
+        nc.vector.memset(spread[:], 0.0)
+        for e in range(2):
+            nc.vector.tensor_copy(out=spread[:, e, :, e], in_=ident[:])
+
+        qs2 = keep.tile([P, D], F32, name="qs2")
+        nc.vector.tensor_scalar(out=qs2[:], in0=qs[:], scalar1=2.0, scalar2=None, op0=ALU.mult)
+        qt2 = keep.tile([P, T], F32, name="qt2")
+        nc.vector.tensor_scalar(out=qt2[:], in0=qt_b[:], scalar1=2.0, scalar2=None, op0=ALU.mult)
+        g_f = keep.tile([P, 8], F32, name="g_f")
+        nc.vector.tensor_copy(out=g_f[:], in_=g_b[:].rearrange("p c j -> p (c j)"))
+
+        k_codes = keep.tile([P, C, 512], U32, name="k_codes", align_bytes=64)
+        k_scales = keep.tile([P, C, 512], U8, name="k_scales", align_bytes=64)
+        v_codes = keep.tile([P, C, 512], U32, name="v_codes", align_bytes=64)
+        v_scales = keep.tile([P, C, 512], U8, name="v_scales", align_bytes=64)
+        q_codes = keep.tile([P, T, P], U32, name="q_codes", align_bytes=64)
+        q_scales = keep.tile([P, T, P], U8, name="q_scales", align_bytes=64)
+        kt_row = keep.tile([P, C, 512], F32, name="kt_row")
+        vt_row = keep.tile([P, C, 512], F32, name="vt_row")
+        ss = keep.tile([P, 8], F32, name="ss")
+        vt16 = keep.tile([P, 8], F32, name="vt16")
+        g_row = psum.tile([P, C, 512], F32, name="g_row", tag="g_row")
+        ymin = keep.tile([P, T], F32, name="ymin")
+        rsum = keep.tile([P, T], F32, name="rsum")
+        rinv = keep.tile([P, T], F32, name="rinv")
+        utr = keep.tile([P, T], F32, name="utr")
+        us2 = keep.tile([P, T], F32, name="us2")
+        sm = keep.tile([P, 4, T], F32, name="sm")
+
+        def broadcast(dst, cols, c):
+            for u in range(2):
+                for e in range(2):
+                    nc.tensor.matmul(
+                        dst[:, 256 * u : 256 * u + 256],
+                        lhsT=cols[:, 4 * c + 2 * u + e : 4 * c + 2 * u + e + 1].to_broadcast([P, P]),
+                        rhs=spread[:, e, :, :].rearrange("p a b -> p (a b)"),
+                        start=(e == 0),
+                        stop=(e == 1),
+                    )
+
+        qf = {}
+        qT = {}
+        kT = {}
+        kg = {}
+        qg = {}
+
+        def q_product(i):
+            pair = i // 2
+            if i % 2 == 0:
+                qf[pair] = work.tile([P, 2, D], BF16, name="qf", tag="qf", bufs=6)
+            nc.vector.tensor_tensor(
+                out=qf[pair][:, i % 2, :], in0=q_raw[:, i, :].bitcast(FP8), in1=qs2[:], op=ALU.mult
+            )
+
+        def q_transpose(pair):
+            qT[pair] = psum.tile([P, 2, 2, P], F32, name="qT", tag="qT")
+            for i2 in range(2):
+                words = qf[pair][:, i2, :].bitcast(F32)
+                for u in range(2):
+                    nc.tensor.transpose(qT[pair][:, i2, u, :], words[:, u : 256 : 2], ident[:])
+
+        def q_interleave(pair):
+            qg[pair] = work.tile([P, 2 * P * 4], BF16, name="qg", tag="qg", align_bytes=64)
+            nc.scalar.copy(
+                out=qg[pair][:].bitcast(F32).rearrange("p (i n u) -> p i n u", i=2, u=2),
+                in_=qT[pair][:].rearrange("p i u n -> p i n u"),
+            )
+
+        def q_quantize(pair):
+            nc.vector.quantize_mx(
+                out=q_codes[:, 2 * pair : 2 * pair + 2, :].rearrange("p i n -> p (i n)").bitcast(FP8X4),
+                scales=q_scales[:, 2 * pair : 2 * pair + 2, :].rearrange("p i n -> p (i n)"),
+                in_=qg[pair][:],
+            )
+
+        def k_transpose(c, u, tag, bufs):
+            kT[c, u] = psum.tile([P, 2, 2, P], F32, name="kT", tag=tag, bufs=bufs)
+            for e in range(2):
+                words = k_raw[:, c, 2 * u + e, :].bitcast(F32)
+                for w in range(2):
+                    nc.tensor.transpose(kT[c, u][:, e, w, :], words[:, w : 256 : 2], ident[:])
+
+        def k_interleave(c, u, copy):
+            if u == 0:
+                kg[c] = work.tile([P, 2048], BF16, name="kg", tag="kg", align_bytes=64)
+            copy(
+                out=kg[c][:, 1024 * u : 1024 * u + 1024].bitcast(F32).rearrange("p (m e w) -> p m e w", e=2, w=2),
+                in_=kT[c, u][:].rearrange("p e w m -> p m e w"),
+            )
+
+        def k_quantize(c):
+            nc.vector.quantize_mx(out=k_codes[:, c, :].bitcast(FP8X4), scales=k_scales[:, c, :], in_=kg[c][:])
+
+        vg = {}
+
+        def value_squares(c):
+            for j in range(4):
+                n = 4 * c + j
+                junk_v = work.tile([P, E], BF16, name="junk_v", tag="junk_s", bufs=2)
+                nc.scalar.activation(
+                    junk_v[:], v_raw[:, c, j, :], ACT.Square, scale=g_f[:, n : n + 1], accum_out=ss[:, n : n + 1]
+                )
+
+        def value_times():
+            vz = keep.tile([P, 8], F32, name="vz")
+            nc.gpsimd.tensor_scalar(
+                out=vz[:], in0=ss[:], scalar1=1.0 / 256.0, scalar2=1.0, op0=ALU.mult, op1=ALU.add
+            )
+            nc.gpsimd.tensor_tensor(out=vt16[:], in0=vz[:], in1=half[:], op=ALU.pow)
+            for c in range(C):
+                vt_ps = psum.tile([P, 2, 2, P], F32, name="vt_ps", tag="us", bufs=2)
+                for u in range(2):
+                    for e in range(2):
+                        n = 4 * c + 2 * u + e
+                        nc.tensor.transpose(vt_ps[:, u, e, :], vt16[:, n : n + 1].to_broadcast([P, P]), ident[:])
+                nc.scalar.copy(
+                    out=vt_row[:, c, :].rearrange("p (u m e) -> p u m e", u=2, e=2),
+                    in_=vt_ps[:].rearrange("p u e m -> p u m e"),
+                )
+
+        def v_interleave(c):
+            vg[c] = work.tile([P, E, 4], BF16, name="vg", tag="vg", align_bytes=64)
+            for h in range(4):
+                cols = slice(128 * h, 128 * h + 128)
+                nc.gpsimd.tensor_scalar(
+                    out=vg[c][:, cols, :],
+                    in0=v_raw[:, c, :, cols].rearrange("p j e -> p e j"),
+                    scalar1=1.0,
+                    scalar2=0.0,
+                    op0=ALU.mult,
+                    op1=ALU.add,
+                )
+
+        def v_quantize(c):
+            nc.vector.quantize_mx(
+                out=v_codes[:, c, :].bitcast(FP8X4),
+                scales=v_scales[:, c, :],
+                in_=vg[c][:].rearrange("p e j -> p (e j)"),
+            )
+
+        S, y, ex, w, pg, pT, pgT, pcodes, pscales, us = {}, {}, {}, {}, {}, {}, {}, {}, {}, {}
+
+        def scores(i):
+            for c in range(C):
+                S[i, c] = psum.tile([P, 512], F32, name="S", tag="S%d" % c)
+                nc.tensor.matmul_mx(
+                    out=S[i, c][:],
+                    lhsT=q_codes[:, i, :].bitcast(FP8X4),
+                    lhsT_scale=q_scales[:, i, :],
+                    rhs=k_codes[:, c, :].bitcast(FP8X4),
+                    rhs_scale=k_scales[:, c, :],
+                    start=True,
+                    stop=True,
+                )
+
+        def distance(i):
+            y[i] = work.tile([P, C, 512], F32, name="y", tag="y")
+            for c in range(C):
+                nc.vector.scalar_tensor_tensor(
+                    out=y[i][:, c, :],
+                    in0=kt_row[:, c, :],
+                    scalar=qt2[:, i : i + 1],
+                    in1=S[i, c][:],
+                    op0=ALU.mult,
+                    op1=ALU.subtract,
+                )
+
+        def minimum(i):
+            nc.vector.tensor_reduce(
+                out=ymin[:, i : i + 1], in_=y[i][:].rearrange("p c m -> p (c m)"), axis=AX.X, op=ALU.min
+            )
+
+        def exponent(i):
+            ex[i] = work.tile([P, C, 512], F32, name="ex", tag="ex", bufs=3)
+            nc.scalar.activation(
+                ex[i][:].rearrange("p c m -> p (c m)"),
+                y[i][:].rearrange("p c m -> p (c m)"),
+                ACT.Exp,
+                bias=ymin[:, i : i + 1],
+                scale=-1.0,
+                accum_out=rsum[:, i : i + 1],
+            )
+
+        def inverse(i):
+            nc.vector.reciprocal(out=rinv[:, i : i + 1], in_=rsum[:, i : i + 1])
+
+        def weights(i):
+            pg[i] = work.tile([P, C, 512], BF16, name="pg", tag="pg")
+            for c in range(C):
+                nc.vector.scalar_tensor_tensor(
+                    out=pg[i][:, c, :],
+                    in0=ex[i][:, c, :],
+                    scalar=rinv[:, i : i + 1],
+                    in1=g_row[:, c, :],
+                    op0=ALU.mult,
+                    op1=ALU.mult,
+                )
+
+        def time_product(i):
+            w[i] = work.tile([P, C, 512], F32, name="w", tag="w")
+            nc.gpsimd.tensor_tensor(out=w[i][:], in0=ex[i][:], in1=vt_row[:], op=ALU.mult)
+
+        def time_vector(i):
+            junk = work.tile([P, C, 512], F32, name="junk_w", tag="junk_w", bufs=1)
+            nc.vector.scalar_tensor_tensor(
+                out=junk[:].rearrange("p c m -> p (c m)"),
+                in0=ex[i][:].rearrange("p c m -> p (c m)"),
+                scalar=1.0,
+                in1=vt_row[:].rearrange("p c m -> p (c m)"),
+                op0=ALU.mult,
+                op1=ALU.mult,
+                accum_out=utr[:, i : i + 1],
+            )
+
+        def time_sum(i):
+            junk = work.tile([P, C, 512], BF16, name="junk_t", tag="junk_t", bufs=1)
+            nc.scalar.activation(
+                junk[:].rearrange("p c m -> p (c m)"),
+                w[i][:].rearrange("p c m -> p (c m)"),
+                ACT.Copy,
+                accum_out=utr[:, i : i + 1],
+            )
+
+        def pg_transpose(i):
+            pT[i] = psum.tile([P, C, 2, P], F32, name="pT", tag="pT")
+            words = pg[i][:].rearrange("p c m -> p (c m)").bitcast(F32)
+            for c in range(C):
+                for u in range(2):
+                    b = 256 * c + 128 * u
+                    nc.tensor.transpose(pT[i][:, c, u, :], words[:, b : b + 128], ident[:])
+
+        def pg_interleave(i):
+            pgT[i] = work.tile([P, C * P * 4], BF16, name="pgT", tag="pgT", align_bytes=64)
+            nc.scalar.copy(
+                out=pgT[i][:].bitcast(F32).rearrange("p (c n u) -> p c n u", c=C, u=2),
+                in_=pT[i][:].rearrange("p c u n -> p c n u"),
+            )
+
+        def pg_quantize(i):
+            pcodes[i] = work.tile([P, C, P], U32, name="pcodes", tag="pcodes", align_bytes=64)
+            pscales[i] = work.tile([P, C, P], U8, name="pscales", tag="pscales", align_bytes=64)
+            nc.vector.quantize_mx(
+                out=pcodes[i][:].rearrange("p c n -> p (c n)").bitcast(FP8X4),
+                scales=pscales[i][:].rearrange("p c n -> p (c n)"),
+                in_=pgT[i][:],
+            )
+
+        def aggregate(i):
+            us[i] = psum.tile([P, E], F32, name="us", tag="us", bufs=2)
+            for c in range(C):
+                nc.tensor.matmul_mx(
+                    out=us[i][:],
+                    lhsT=pcodes[i][:, c, :].bitcast(FP8X4),
+                    lhsT_scale=pscales[i][:, c, :],
+                    rhs=v_codes[:, c, :].bitcast(FP8X4),
+                    rhs_scale=v_scales[:, c, :],
+                    start=(c == 0),
+                    stop=(c == C - 1),
+                )
+
+        def square_sum(i):
+            junk = work.tile([P, E], BF16, name="junk_s", tag="junk_s", bufs=2)
+            nc.scalar.activation(junk[:], us[i][:], ACT.Square, scale=1.0 / 16.0, accum_out=us2[:, i : i + 1])
+
+        def root_time(i):
+            a, a2 = (sm[:, n, i : i + 1] for n in range(2))
+            nc.gpsimd.tensor_tensor(out=a, in0=utr[:, i : i + 1], in1=rinv[:, i : i + 1], op=ALU.mult)
+            nc.gpsimd.tensor_tensor(out=a2, in0=a, in1=a, op=ALU.mult)
+
+        def root(i):
+            a2, z, r = (sm[:, n, i : i + 1] for n in range(1, 4))
+            nc.gpsimd.tensor_tensor(out=z, in0=a2, in1=us2[:, i : i + 1], op=ALU.subtract)
+            nc.gpsimd.tensor_tensor(out=r, in0=z, in1=nhalf[:], op=ALU.pow)
+
+        out_view = out.rearrange("(p i) e -> p i e", i=T)
+
+        def finish(i):
+            o = work.tile([P, E], F32, name="o", tag="o", bufs=3)
+            nc.scalar.activation(o[:], us[i][:], ACT.Copy, scale=sm[:, 3, i : i + 1])
+            nc.sync.dma_start(out=out_view[:, i, :], in_=o[:])
+
+        kt_ps = {}
+        for c in range(C):
+            kt_ps[c] = psum.tile([P, 512], F32, name="kt_ps", tag="S%d" % c)
+            broadcast(kt_ps[c], kt_b[:].rearrange("p c j -> p (c j)"), c)
+        k_transpose(0, 0, "us", 2)
+        k_interleave(0, 0, nc.scalar.copy)
+        q_product(0)
+        q_product(1)
+        for c in range(C):
+            nc.vector.tensor_copy(out=kt_row[:, c, :], in_=kt_ps[c][:])
+        k_transpose(0, 1, "us", 2)
+        k_interleave(0, 1, nc.scalar.copy)
+        q_transpose(0)
+        q_interleave(0)
+        k_transpose(1, 0, "pT", None)
+        k_interleave(1, 0, nc.vector.tensor_copy)
+        k_quantize(0)
+        k_transpose(1, 1, "us", 2)
+        k_interleave(1, 1, nc.scalar.copy)
+        q_quantize(0)
+        q_product(2)
+        k_quantize(1)
+        scores(0)
+        for c in range(C):
+            broadcast(g_row[:, c, :], g_b[:].rearrange("p c j -> p (c j)"), c)
+        value_squares(0)
+        value_squares(1)
+
+        for i in range(T + 3):
+            if i < T:
+                distance(i)
+            if i + 1 < T and i != 1:
+                scores(i + 1)
+            if 0 <= i - 2 < T:
+                square_sum(i - 2)
+                root(i - 2)
+            if 0 <= i - 3 < T:
+                finish(i - 3)
+            if 0 <= i - 1 < T:
+                inverse(i - 1)
+                weights(i - 1)
+                pg_transpose(i - 1)
+                pg_interleave(i - 1)
+            if i % 2 == 1 and (i + 3) // 2 < T // 2 and i > 1:
+                q_transpose((i + 3) // 2)
+                q_interleave((i + 3) // 2)
+            if i < T:
+                minimum(i)
+                exponent(i)
+            if i == 0:
+                q_product(3)
+                q_transpose(1)
+                q_interleave(1)
+                v_interleave(0)
+                value_times()
+                v_interleave(1)
+            if i == 1:
+                q_quantize(1)
+                scores(2)
+                q_product(4)
+                q_product(5)
+                q_transpose(2)
+                q_interleave(2)
+            if i < T and i not in UT_ON_VECTOR:
+                time_product(i)
+            if 0 <= i - 1 < T:
+                if i - 1 in UT_ON_VECTOR:
+                    time_vector(i - 1)
+                else:
+                    time_sum(i - 1)
+                root_time(i - 1)
+            if i + 6 < T:
+                q_product(i + 6)
+            if i == 1:
+                v_quantize(0)
+                v_quantize(1)
+            if 0 <= i - 1 < T:
+                pg_quantize(i - 1)
+            if i > 0 and i % 2 == 0 and i // 2 + 1 < T // 2:
+                q_quantize(i // 2 + 1)
+            if 0 <= i - 1 < T:
+                aggregate(i - 1)

@@ -18,7 +18,6 @@ AX = mybir.AxisListType
 
 P = 128
 T = N // P
-UT_ON_VECTOR = (15,)
 C = M // 512
 
 
@@ -48,8 +47,8 @@ def tile_lorentzcentroidaggregation_kernel(tc, q_bytes, q_scale, qt, k, kt, v, g
         nc.sync.dma_start(out=qs[:], in_=q_scale.rearrange("o d -> (o d)").partition_broadcast(P))
         nc.sync.dma_start(out=q_raw[:, 0:2, :], in_=q_view[:, 0:2, :])
         nc.sync.dma_start(out=k_raw[:, 0, 2:4, :], in_=k_view[:, 0, 2:4, :])
-        nc.sync.dma_start(out=k_raw[:, 1, :, :], in_=k_view[:, 1, :, :])
         nc.sync.dma_start(out=q_raw[:, 2:8, :], in_=q_view[:, 2:8, :])
+        nc.sync.dma_start(out=k_raw[:, 1, :, :], in_=k_view[:, 1, :, :])
         nc.sync.dma_start(out=v_raw[:, 0, :, :], in_=v_view[:, 0, :, :])
         nc.sync.dma_start(out=v_raw[:, 1, :, :], in_=v_view[:, 1, :, :])
         nc.sync.dma_start(out=q_raw[:, 8:16, :], in_=q_view[:, 8:16, :])
@@ -91,9 +90,9 @@ def tile_lorentzcentroidaggregation_kernel(tc, q_bytes, q_scale, qt, k, kt, v, g
         ymin = keep.tile([P, T], F32, name="ymin")
         rsum = keep.tile([P, T], F32, name="rsum")
         rinv = keep.tile([P, T], F32, name="rinv")
-        utr = keep.tile([P, T], F32, name="utr")
+        ut = keep.tile([P, T], F32, name="ut")
         us2 = keep.tile([P, T], F32, name="us2")
-        sm = keep.tile([P, 4, T], F32, name="sm")
+        sm = keep.tile([P, 2, T], F32, name="sm")
 
         def broadcast(dst, cols, c):
             for u in range(2):
@@ -115,7 +114,7 @@ def tile_lorentzcentroidaggregation_kernel(tc, q_bytes, q_scale, qt, k, kt, v, g
         def q_product(i):
             pair = i // 2
             if i % 2 == 0:
-                qf[pair] = work.tile([P, 2, D], BF16, name="qf", tag="qf", bufs=6)
+                qf[pair] = work.tile([P, 2, D], BF16, name="qf", tag="qf", bufs=8)
             nc.vector.tensor_tensor(
                 out=qf[pair][:, i % 2, :], in0=q_raw[:, i, :].bitcast(FP8), in1=qs2[:], op=ALU.mult
             )
@@ -208,18 +207,21 @@ def tile_lorentzcentroidaggregation_kernel(tc, q_bytes, q_scale, qt, k, kt, v, g
 
         S, y, ex, w, pg, pT, pgT, pcodes, pscales, us = {}, {}, {}, {}, {}, {}, {}, {}, {}, {}
 
+        def scores_part(i, c):
+            S[i, c] = psum.tile([P, 512], F32, name="S", tag="S%d" % c)
+            nc.tensor.matmul_mx(
+                out=S[i, c][:],
+                lhsT=q_codes[:, i, :].bitcast(FP8X4),
+                lhsT_scale=q_scales[:, i, :],
+                rhs=k_codes[:, c, :].bitcast(FP8X4),
+                rhs_scale=k_scales[:, c, :],
+                start=True,
+                stop=True,
+            )
+
         def scores(i):
             for c in range(C):
-                S[i, c] = psum.tile([P, 512], F32, name="S", tag="S%d" % c)
-                nc.tensor.matmul_mx(
-                    out=S[i, c][:],
-                    lhsT=q_codes[:, i, :].bitcast(FP8X4),
-                    lhsT_scale=q_scales[:, i, :],
-                    rhs=k_codes[:, c, :].bitcast(FP8X4),
-                    rhs_scale=k_scales[:, c, :],
-                    start=True,
-                    stop=True,
-                )
+                scores_part(i, c)
 
         def distance(i):
             y[i] = work.tile([P, C, 512], F32, name="y", tag="y")
@@ -239,7 +241,7 @@ def tile_lorentzcentroidaggregation_kernel(tc, q_bytes, q_scale, qt, k, kt, v, g
             )
 
         def exponent(i):
-            ex[i] = work.tile([P, C, 512], F32, name="ex", tag="ex", bufs=3)
+            ex[i] = work.tile([P, C, 512], F32, name="ex", tag="ex", bufs=4)
             nc.scalar.activation(
                 ex[i][:].rearrange("p c m -> p (c m)"),
                 y[i][:].rearrange("p c m -> p (c m)"),
@@ -273,11 +275,11 @@ def tile_lorentzcentroidaggregation_kernel(tc, q_bytes, q_scale, qt, k, kt, v, g
             nc.vector.scalar_tensor_tensor(
                 out=junk[:].rearrange("p c m -> p (c m)"),
                 in0=ex[i][:].rearrange("p c m -> p (c m)"),
-                scalar=1.0,
+                scalar=rinv[:, i : i + 1],
                 in1=vt_row[:].rearrange("p c m -> p (c m)"),
                 op0=ALU.mult,
                 op1=ALU.mult,
-                accum_out=utr[:, i : i + 1],
+                accum_out=ut[:, i : i + 1],
             )
 
         def time_sum(i):
@@ -286,11 +288,12 @@ def tile_lorentzcentroidaggregation_kernel(tc, q_bytes, q_scale, qt, k, kt, v, g
                 junk[:].rearrange("p c m -> p (c m)"),
                 w[i][:].rearrange("p c m -> p (c m)"),
                 ACT.Copy,
-                accum_out=utr[:, i : i + 1],
+                scale=rinv[:, i : i + 1],
+                accum_out=ut[:, i : i + 1],
             )
 
-        def pg_transpose(i):
-            pT[i] = psum.tile([P, C, 2, P], F32, name="pT", tag="pT")
+        def pg_transpose(i, tag="pT"):
+            pT[i] = psum.tile([P, C, 2, P], F32, name="pT", tag=tag)
             words = pg[i][:].rearrange("p c m -> p (c m)").bitcast(F32)
             for c in range(C):
                 for u in range(2):
@@ -313,8 +316,8 @@ def tile_lorentzcentroidaggregation_kernel(tc, q_bytes, q_scale, qt, k, kt, v, g
                 in_=pgT[i][:],
             )
 
-        def aggregate(i):
-            us[i] = psum.tile([P, E], F32, name="us", tag="us", bufs=2)
+        def aggregate(i, tag="us", bufs=2):
+            us[i] = psum.tile([P, E], F32, name="us", tag=tag, bufs=bufs)
             for c in range(C):
                 nc.tensor.matmul_mx(
                     out=us[i][:],
@@ -330,21 +333,26 @@ def tile_lorentzcentroidaggregation_kernel(tc, q_bytes, q_scale, qt, k, kt, v, g
             junk = work.tile([P, E], BF16, name="junk_s", tag="junk_s", bufs=2)
             nc.scalar.activation(junk[:], us[i][:], ACT.Square, scale=1.0 / 16.0, accum_out=us2[:, i : i + 1])
 
-        def root_time(i):
-            a, a2 = (sm[:, n, i : i + 1] for n in range(2))
-            nc.gpsimd.tensor_tensor(out=a, in0=utr[:, i : i + 1], in1=rinv[:, i : i + 1], op=ALU.mult)
-            nc.gpsimd.tensor_tensor(out=a2, in0=a, in1=a, op=ALU.mult)
-
         def root(i):
-            a2, z, r = (sm[:, n, i : i + 1] for n in range(1, 4))
-            nc.gpsimd.tensor_tensor(out=z, in0=a2, in1=us2[:, i : i + 1], op=ALU.subtract)
+            z, r = (sm[:, n, i : i + 1] for n in range(2))
+            nc.gpsimd.tensor_scalar(
+                out=z,
+                in0=ut[:, i : i + 1],
+                scalar1=ut[:, i : i + 1],
+                scalar2=us2[:, i : i + 1],
+                op0=ALU.mult,
+                op1=ALU.subtract,
+            )
             nc.gpsimd.tensor_tensor(out=r, in0=z, in1=nhalf[:], op=ALU.pow)
 
         out_view = out.rearrange("(p i) e -> p i e", i=T)
 
-        def finish(i):
+        def finish(i, on_vector=False):
             o = work.tile([P, E], F32, name="o", tag="o", bufs=3)
-            nc.scalar.activation(o[:], us[i][:], ACT.Copy, scale=sm[:, 3, i : i + 1])
+            if on_vector:
+                nc.vector.tensor_scalar(out=o[:], in0=us[i][:], scalar1=sm[:, 1, i : i + 1], scalar2=None, op0=ALU.mult)
+            else:
+                nc.scalar.activation(o[:], us[i][:], ACT.Copy, scale=sm[:, 1, i : i + 1])
             nc.sync.dma_start(out=out_view[:, i, :], in_=o[:])
 
         kt_ps = {}
@@ -355,77 +363,105 @@ def tile_lorentzcentroidaggregation_kernel(tc, q_bytes, q_scale, qt, k, kt, v, g
         k_interleave(0, 0, nc.scalar.copy)
         q_product(0)
         q_product(1)
-        for c in range(C):
-            nc.vector.tensor_copy(out=kt_row[:, c, :], in_=kt_ps[c][:])
         k_transpose(0, 1, "us", 2)
         k_interleave(0, 1, nc.scalar.copy)
+        for c in range(C):
+            nc.vector.tensor_copy(out=kt_row[:, c, :], in_=kt_ps[c][:])
         q_transpose(0)
         q_interleave(0)
         k_transpose(1, 0, "pT", None)
-        k_interleave(1, 0, nc.vector.tensor_copy)
+        k_interleave(1, 0, nc.scalar.copy)
+        for i in range(2, 6):
+            q_product(i)
         k_quantize(0)
+        q_quantize(0)
+        scores_part(0, 0)
         k_transpose(1, 1, "us", 2)
         k_interleave(1, 1, nc.scalar.copy)
-        q_quantize(0)
-        q_product(2)
+        q_transpose(1)
+        q_interleave(1)
+        q_product(6)
+        q_product(7)
         k_quantize(1)
-        scores(0)
-        for c in range(C):
-            broadcast(g_row[:, c, :], g_b[:].rearrange("p c j -> p (c j)"), c)
+        scores_part(0, 1)
+        q_quantize(1)
         value_squares(0)
         value_squares(1)
 
-        for i in range(T + 3):
-            if i < T:
-                distance(i)
-            if i + 1 < T and i != 1:
+        for i in range(T):
+            distance(i)
+            if i + 1 < T:
                 scores(i + 1)
-            if 0 <= i - 2 < T:
-                square_sum(i - 2)
-                root(i - 2)
-            if 0 <= i - 3 < T:
-                finish(i - 3)
-            if 0 <= i - 1 < T:
-                inverse(i - 1)
-                weights(i - 1)
-                pg_transpose(i - 1)
-                pg_interleave(i - 1)
-            if i % 2 == 1 and (i + 3) // 2 < T // 2 and i > 1:
-                q_transpose((i + 3) // 2)
-                q_interleave((i + 3) // 2)
-            if i < T:
-                minimum(i)
-                exponent(i)
             if i == 0:
-                q_product(3)
-                q_transpose(1)
-                q_interleave(1)
+                for c in range(C):
+                    broadcast(g_row[:, c, :], g_b[:].rearrange("p c j -> p (c j)"), c)
+            if i >= 1:
+                inverse(i - 1)
+            if i >= 3:
+                pg_interleave(i - 3)
+            if i > 0 and i % 2 == 0 and i // 2 + 1 < T // 2:
+                q_interleave(i // 2 + 1)
+            if i >= 2:
+                time_sum(i - 2)
+            if i >= 4:
+                square_sum(i - 4)
+                root(i - 4)
+            if i >= 5:
+                finish(i - 5)
+            if i >= 2:
+                weights(i - 2)
+                pg_transpose(i - 2)
+            if i % 2 == 1 and (i + 3) // 2 < T // 2:
+                q_transpose((i + 3) // 2)
+            minimum(i)
+            exponent(i)
+            if i == 0:
+                q_product(8)
                 v_interleave(0)
-                value_times()
                 v_interleave(1)
             if i == 1:
-                q_quantize(1)
-                scores(2)
-                q_product(4)
-                q_product(5)
-                q_transpose(2)
-                q_interleave(2)
-            if i < T and i not in UT_ON_VECTOR:
+                value_times()
+                time_product(0)
+            if 1 <= i < T - 2:
                 time_product(i)
-            if 0 <= i - 1 < T:
-                if i - 1 in UT_ON_VECTOR:
-                    time_vector(i - 1)
-                else:
-                    time_sum(i - 1)
-                root_time(i - 1)
-            if i + 6 < T:
-                q_product(i + 6)
+            if 1 <= i < T - 8:
+                q_product(i + 8)
             if i == 1:
                 v_quantize(0)
                 v_quantize(1)
-            if 0 <= i - 1 < T:
-                pg_quantize(i - 1)
+            if i >= 3:
+                pg_quantize(i - 3)
             if i > 0 and i % 2 == 0 and i // 2 + 1 < T // 2:
                 q_quantize(i // 2 + 1)
-            if 0 <= i - 1 < T:
-                aggregate(i - 1)
+            if i >= 3:
+                aggregate(i - 3)
+
+        weights(T - 2)
+        pg_interleave(T - 3)
+        pg_transpose(T - 2)
+        pg_quantize(T - 3)
+        aggregate(T - 3)
+        square_sum(T - 4)
+        root(T - 4)
+        time_vector(T - 2)
+        pg_interleave(T - 2)
+        inverse(T - 1)
+        weights(T - 1)
+        pg_transpose(T - 1, "qT")
+        pg_quantize(T - 2)
+        aggregate(T - 2, "S0", None)
+        finish(T - 5)
+        square_sum(T - 3)
+        root(T - 3)
+        pg_interleave(T - 1)
+        time_vector(T - 1)
+        pg_quantize(T - 1)
+        aggregate(T - 1, "S1", None)
+        square_sum(T - 2)
+        root(T - 2)
+        finish(T - 4)
+        finish(T - 3, on_vector=True)
+        square_sum(T - 1)
+        root(T - 1)
+        finish(T - 2, on_vector=True)
+        finish(T - 1)

@@ -56,7 +56,11 @@ def tile_lorentzcentroidaggregation_kernel(tc, q_bytes, q_scale, qt, k, kt, v, g
         ident = keep.tile([P, P], F32, name="ident")
         make_identity(nc, ident[:])
         half = keep.tile([P, 8], F32, name="half")
-        nhalf = keep.tile([P, 1], F32, name="nhalf")
+        nhalf = keep.tile([P, 2], F32, name="nhalf")
+        minus1 = keep.tile([P, 1], F32, name="minus1")
+        ones = keep.tile([P, 1], F32, name="ones")
+        nc.gpsimd.memset(minus1[:], -1.0)
+        nc.gpsimd.memset(ones[:], 1.0)
         nc.gpsimd.memset(half[:], 0.5)
         nc.gpsimd.memset(nhalf[:], -0.5)
         warm = keep.tile([P, 1], F32, name="warm")
@@ -69,8 +73,9 @@ def tile_lorentzcentroidaggregation_kernel(tc, q_bytes, q_scale, qt, k, kt, v, g
         for e in range(2):
             nc.vector.tensor_copy(out=spread[:, e, :, e], in_=ident[:])
 
-        qs2 = keep.tile([P, D], F32, name="qs2")
-        nc.vector.tensor_scalar(out=qs2[:], in0=qs[:], scalar1=2.0, scalar2=None, op0=ALU.mult)
+        qs2 = keep.tile([P, 2, D], F32, name="qs2")
+        for h in range(2):
+            nc.vector.tensor_scalar(out=qs2[:, h, :], in0=qs[:], scalar1=2.0, scalar2=None, op0=ALU.mult)
         qt2 = keep.tile([P, T], F32, name="qt2")
         nc.vector.tensor_scalar(out=qt2[:], in0=qt_b[:], scalar1=2.0, scalar2=None, op0=ALU.mult)
         g_f = keep.tile([P, 8], F32, name="g_f")
@@ -86,13 +91,13 @@ def tile_lorentzcentroidaggregation_kernel(tc, q_bytes, q_scale, qt, k, kt, v, g
         vt_row = keep.tile([P, C, 512], F32, name="vt_row")
         ss = keep.tile([P, 8], F32, name="ss")
         vt16 = keep.tile([P, 8], F32, name="vt16")
-        g_row = psum.tile([P, C, 512], F32, name="g_row", tag="g_row")
+        g_row = psum.tile([P, C, 512], BF16, name="g_row", tag="g_row")
         ymin = keep.tile([P, T], F32, name="ymin")
         rsum = keep.tile([P, T], F32, name="rsum")
         rinv = keep.tile([P, T], F32, name="rinv")
         ut = keep.tile([P, T], F32, name="ut")
         us2 = keep.tile([P, T], F32, name="us2")
-        sm = keep.tile([P, 2, T], F32, name="sm")
+        sm = keep.tile([P, 3, T], F32, name="sm")
 
         def broadcast(dst, cols, c):
             for u in range(2):
@@ -111,12 +116,13 @@ def tile_lorentzcentroidaggregation_kernel(tc, q_bytes, q_scale, qt, k, kt, v, g
         kg = {}
         qg = {}
 
-        def q_product(i):
-            pair = i // 2
-            if i % 2 == 0:
-                qf[pair] = work.tile([P, 2, D], BF16, name="qf", tag="qf", bufs=8)
+        def q_product(pair):
+            qf[pair] = work.tile([P, 2, D], BF16, name="qf", tag="qf", bufs=5)
             nc.vector.tensor_tensor(
-                out=qf[pair][:, i % 2, :], in0=q_raw[:, i, :].bitcast(FP8), in1=qs2[:], op=ALU.mult
+                out=qf[pair][:].rearrange("p i d -> p (i d)"),
+                in0=q_raw[:, 2 * pair : 2 * pair + 2, :].rearrange("p i d -> p (i d)").bitcast(FP8),
+                in1=qs2[:].rearrange("p i d -> p (i d)"),
+                op=ALU.mult,
             )
 
         def q_transpose(pair):
@@ -127,17 +133,19 @@ def tile_lorentzcentroidaggregation_kernel(tc, q_bytes, q_scale, qt, k, kt, v, g
                     nc.tensor.transpose(qT[pair][:, i2, u, :], words[:, u : 256 : 2], ident[:])
 
         def q_interleave(pair):
-            qg[pair] = work.tile([P, 2 * P * 4], BF16, name="qg", tag="qg", align_bytes=64)
+            if pair % 2 == 0:
+                qg[pair // 2] = work.tile([P, 2, 2 * P * 4], BF16, name="qg", tag="qg", align_bytes=64)
             nc.scalar.copy(
-                out=qg[pair][:].bitcast(F32).rearrange("p (i n u) -> p i n u", i=2, u=2),
+                out=qg[pair // 2][:, pair % 2, :].bitcast(F32).rearrange("p (i n u) -> p i n u", i=2, u=2),
                 in_=qT[pair][:].rearrange("p i u n -> p i n u"),
             )
 
-        def q_quantize(pair):
+        def q_quantize(pair, pairs):
+            tiles = slice(2 * pair, 2 * (pair + pairs))
             nc.vector.quantize_mx(
-                out=q_codes[:, 2 * pair : 2 * pair + 2, :].rearrange("p i n -> p (i n)").bitcast(FP8X4),
-                scales=q_scales[:, 2 * pair : 2 * pair + 2, :].rearrange("p i n -> p (i n)"),
-                in_=qg[pair][:],
+                out=q_codes[:, tiles, :].rearrange("p i n -> p (i n)").bitcast(FP8X4),
+                scales=q_scales[:, tiles, :].rearrange("p i n -> p (i n)"),
+                in_=qg[pair // 2][:, pair % 2 : pair % 2 + pairs, :].rearrange("p a b -> p (a b)"),
             )
 
         def k_transpose(c, u, tag, bufs):
@@ -174,6 +182,8 @@ def tile_lorentzcentroidaggregation_kernel(tc, q_bytes, q_scale, qt, k, kt, v, g
                 out=vz[:], in0=ss[:], scalar1=1.0 / 256.0, scalar2=1.0, op0=ALU.mult, op1=ALU.add
             )
             nc.gpsimd.tensor_tensor(out=vt16[:], in0=vz[:], in1=half[:], op=ALU.pow)
+
+        def value_rows():
             for c in range(C):
                 vt_ps = psum.tile([P, 2, 2, P], F32, name="vt_ps", tag="us", bufs=2)
                 for u in range(2):
@@ -223,9 +233,9 @@ def tile_lorentzcentroidaggregation_kernel(tc, q_bytes, q_scale, qt, k, kt, v, g
             for c in range(C):
                 scores_part(i, c)
 
-        def distance(i):
-            y[i] = work.tile([P, C, 512], F32, name="y", tag="y")
-            for c in range(C):
+        def distance_part(i, c):
+                if c == 0:
+                    y[i] = work.tile([P, C, 512], F32, name="y", tag="y")
                 nc.vector.scalar_tensor_tensor(
                     out=y[i][:, c, :],
                     in0=kt_row[:, c, :],
@@ -235,13 +245,17 @@ def tile_lorentzcentroidaggregation_kernel(tc, q_bytes, q_scale, qt, k, kt, v, g
                     op1=ALU.subtract,
                 )
 
+        def distance(i):
+            for c in range(C):
+                distance_part(i, c)
+
         def minimum(i):
             nc.vector.tensor_reduce(
                 out=ymin[:, i : i + 1], in_=y[i][:].rearrange("p c m -> p (c m)"), axis=AX.X, op=ALU.min
             )
 
         def exponent(i):
-            ex[i] = work.tile([P, C, 512], F32, name="ex", tag="ex", bufs=4)
+            ex[i] = work.tile([P, C, 512], F32, name="ex", tag="ex", bufs=6)
             nc.scalar.activation(
                 ex[i][:].rearrange("p c m -> p (c m)"),
                 y[i][:].rearrange("p c m -> p (c m)"),
@@ -252,26 +266,25 @@ def tile_lorentzcentroidaggregation_kernel(tc, q_bytes, q_scale, qt, k, kt, v, g
             )
 
         def inverse(i):
-            nc.vector.reciprocal(out=rinv[:, i : i + 1], in_=rsum[:, i : i + 1])
+            nc.gpsimd.tensor_tensor(out=rinv[:, i : i + 1], in0=rsum[:, i : i + 1], in1=minus1[:], op=ALU.pow)
 
         def weights(i):
             pg[i] = work.tile([P, C, 512], BF16, name="pg", tag="pg")
-            for c in range(C):
-                nc.vector.scalar_tensor_tensor(
-                    out=pg[i][:, c, :],
-                    in0=ex[i][:, c, :],
-                    scalar=rinv[:, i : i + 1],
-                    in1=g_row[:, c, :],
-                    op0=ALU.mult,
-                    op1=ALU.mult,
-                )
+            nc.vector.scalar_tensor_tensor(
+                out=pg[i][:].rearrange("p c m -> p (c m)"),
+                in0=ex[i][:].rearrange("p c m -> p (c m)"),
+                scalar=rinv[:, i : i + 1],
+                in1=g_row[:].rearrange("p c m -> p (c m)"),
+                op0=ALU.mult,
+                op1=ALU.mult,
+            )
 
         def time_product(i):
-            w[i] = work.tile([P, C, 512], F32, name="w", tag="w")
+            w[i] = work.tile([P, C, 512], F32, name="w", tag="w", bufs=4)
             nc.gpsimd.tensor_tensor(out=w[i][:], in0=ex[i][:], in1=vt_row[:], op=ALU.mult)
 
         def time_vector(i):
-            junk = work.tile([P, C, 512], F32, name="junk_w", tag="junk_w", bufs=1)
+            junk = work.tile([P, C, 512], BF16, name="junk_w", tag="junk_w", bufs=1)
             nc.vector.scalar_tensor_tensor(
                 out=junk[:].rearrange("p c m -> p (c m)"),
                 in0=ex[i][:].rearrange("p c m -> p (c m)"),
@@ -282,15 +295,36 @@ def tile_lorentzcentroidaggregation_kernel(tc, q_bytes, q_scale, qt, k, kt, v, g
                 accum_out=ut[:, i : i + 1],
             )
 
-        def time_sum(i):
-            junk = work.tile([P, C, 512], BF16, name="junk_t", tag="junk_t", bufs=1)
-            nc.scalar.activation(
-                junk[:].rearrange("p c m -> p (c m)"),
-                w[i][:].rearrange("p c m -> p (c m)"),
-                ACT.Copy,
-                scale=rinv[:, i : i + 1],
-                accum_out=ut[:, i : i + 1],
-            )
+        wT, ws = {}, {}
+
+        def time_fold(i):
+            if i % 2 == 0:
+                wT[i // 2] = psum.tile([P, 3, P], F32, name="wT", tag="wT")
+            flat = w[i][:].rearrange("p c m -> p (c m)")
+            for b in range(8):
+                nc.tensor.matmul(
+                    wT[i // 2][:, i % 2, :],
+                    lhsT=flat[:, P * b : P * b + P],
+                    rhs=ident[:],
+                    is_transpose=True,
+                    start=(b == 0),
+                    stop=(b == 7),
+                )
+
+        def time_copy(pair):
+            ws[pair] = work.tile([P, 2, P], F32, name="ws", tag="ws")
+            nc.scalar.copy(out=ws[pair][:], in_=wT[pair][:, 0:2, :])
+
+        def time_total(pair):
+            for h in range(2):
+                nc.tensor.matmul(
+                    wT[pair][:, 2, h : h + 1], lhsT=ws[pair][:, h, :], rhs=ones[:], start=True, stop=True
+                )
+
+        def time_scale(pair):
+            for h in range(2):
+                i = 2 * pair + h
+                nc.scalar.activation(ut[:, i : i + 1], wT[pair][:, 2, h : h + 1], ACT.Copy, scale=rinv[:, i : i + 1])
 
         def pg_transpose(i, tag="pT"):
             pT[i] = psum.tile([P, C, 2, P], F32, name="pT", tag=tag)
@@ -301,19 +335,22 @@ def tile_lorentzcentroidaggregation_kernel(tc, q_bytes, q_scale, qt, k, kt, v, g
                     nc.tensor.transpose(pT[i][:, c, u, :], words[:, b : b + 128], ident[:])
 
         def pg_interleave(i):
-            pgT[i] = work.tile([P, C * P * 4], BF16, name="pgT", tag="pgT", align_bytes=64)
+            if i % 2 == 0:
+                pgT[i // 2] = work.tile([P, 2, C * P * 4], BF16, name="pgT", tag="pgT", align_bytes=64)
             nc.scalar.copy(
-                out=pgT[i][:].bitcast(F32).rearrange("p (c n u) -> p c n u", c=C, u=2),
+                out=pgT[i // 2][:, i % 2, :].bitcast(F32).rearrange("p (c n u) -> p c n u", c=C, u=2),
                 in_=pT[i][:].rearrange("p c u n -> p c n u"),
             )
 
-        def pg_quantize(i):
-            pcodes[i] = work.tile([P, C, P], U32, name="pcodes", tag="pcodes", align_bytes=64)
-            pscales[i] = work.tile([P, C, P], U8, name="pscales", tag="pscales", align_bytes=64)
+        def pg_quantize(i, tiles):
+            if i % 2 == 0:
+                pcodes[i // 2] = work.tile([P, 2, C, P], U32, name="pcodes", tag="pcodes", align_bytes=64)
+                pscales[i // 2] = work.tile([P, 2, C, P], U8, name="pscales", tag="pscales", align_bytes=64)
+            part = slice(i % 2, i % 2 + tiles)
             nc.vector.quantize_mx(
-                out=pcodes[i][:].rearrange("p c n -> p (c n)").bitcast(FP8X4),
-                scales=pscales[i][:].rearrange("p c n -> p (c n)"),
-                in_=pgT[i][:],
+                out=pcodes[i // 2][:, part, :, :].rearrange("p i c n -> p (i c n)").bitcast(FP8X4),
+                scales=pscales[i // 2][:, part, :, :].rearrange("p i c n -> p (i c n)"),
+                in_=pgT[i // 2][:, part, :].rearrange("p i x -> p (i x)"),
             )
 
         def aggregate(i, tag="us", bufs=2):
@@ -321,8 +358,8 @@ def tile_lorentzcentroidaggregation_kernel(tc, q_bytes, q_scale, qt, k, kt, v, g
             for c in range(C):
                 nc.tensor.matmul_mx(
                     out=us[i][:],
-                    lhsT=pcodes[i][:, c, :].bitcast(FP8X4),
-                    lhsT_scale=pscales[i][:, c, :],
+                    lhsT=pcodes[i // 2][:, i % 2, c, :].bitcast(FP8X4),
+                    lhsT_scale=pscales[i // 2][:, i % 2, c, :],
                     rhs=v_codes[:, c, :].bitcast(FP8X4),
                     rhs_scale=v_scales[:, c, :],
                     start=(c == 0),
@@ -333,26 +370,23 @@ def tile_lorentzcentroidaggregation_kernel(tc, q_bytes, q_scale, qt, k, kt, v, g
             junk = work.tile([P, E], BF16, name="junk_s", tag="junk_s", bufs=2)
             nc.scalar.activation(junk[:], us[i][:], ACT.Square, scale=1.0 / 16.0, accum_out=us2[:, i : i + 1])
 
-        def root(i):
-            z, r = (sm[:, n, i : i + 1] for n in range(2))
-            nc.gpsimd.tensor_scalar(
-                out=z,
-                in0=ut[:, i : i + 1],
-                scalar1=ut[:, i : i + 1],
-                scalar2=us2[:, i : i + 1],
-                op0=ALU.mult,
-                op1=ALU.subtract,
-            )
-            nc.gpsimd.tensor_tensor(out=r, in0=z, in1=nhalf[:], op=ALU.pow)
+        def root_square(i, tiles=2):
+            cols = slice(i, i + tiles)
+            nc.gpsimd.tensor_tensor(out=sm[:, 0, cols], in0=ut[:, cols], in1=ut[:, cols], op=ALU.mult)
+
+        def root(i, tiles=2):
+            cols = slice(i, i + tiles)
+            nc.gpsimd.tensor_tensor(out=sm[:, 1, cols], in0=sm[:, 0, cols], in1=us2[:, cols], op=ALU.subtract)
+            nc.gpsimd.tensor_tensor(out=sm[:, 2, cols], in0=sm[:, 1, cols], in1=nhalf[:, 0:tiles], op=ALU.pow)
 
         out_view = out.rearrange("(p i) e -> p i e", i=T)
 
         def finish(i, on_vector=False):
             o = work.tile([P, E], F32, name="o", tag="o", bufs=3)
             if on_vector:
-                nc.vector.tensor_scalar(out=o[:], in0=us[i][:], scalar1=sm[:, 1, i : i + 1], scalar2=None, op0=ALU.mult)
+                nc.vector.tensor_scalar(out=o[:], in0=us[i][:], scalar1=sm[:, 2, i : i + 1], scalar2=None, op0=ALU.mult)
             else:
-                nc.scalar.activation(o[:], us[i][:], ACT.Copy, scale=sm[:, 1, i : i + 1])
+                nc.scalar.activation(o[:], us[i][:], ACT.Copy, scale=sm[:, 2, i : i + 1])
             nc.sync.dma_start(out=out_view[:, i, :], in_=o[:])
 
         kt_ps = {}
@@ -362,106 +396,136 @@ def tile_lorentzcentroidaggregation_kernel(tc, q_bytes, q_scale, qt, k, kt, v, g
         k_transpose(0, 0, "us", 2)
         k_interleave(0, 0, nc.scalar.copy)
         q_product(0)
-        q_product(1)
         k_transpose(0, 1, "us", 2)
         k_interleave(0, 1, nc.scalar.copy)
-        for c in range(C):
-            nc.vector.tensor_copy(out=kt_row[:, c, :], in_=kt_ps[c][:])
         q_transpose(0)
         q_interleave(0)
         k_transpose(1, 0, "pT", None)
         k_interleave(1, 0, nc.scalar.copy)
-        for i in range(2, 6):
-            q_product(i)
-        k_quantize(0)
-        q_quantize(0)
-        scores_part(0, 0)
+        q_product(1)
+        for c in range(C):
+            nc.scalar.copy(out=kt_row[:, c, :], in_=kt_ps[c][:])
         k_transpose(1, 1, "us", 2)
         k_interleave(1, 1, nc.scalar.copy)
+        q_product(2)
+        k_quantize(0)
+        q_quantize(0, 1)
+        scores_part(0, 0)
         q_transpose(1)
         q_interleave(1)
-        q_product(6)
-        q_product(7)
+        q_product(3)
+        distance_part(0, 0)
         k_quantize(1)
         scores_part(0, 1)
-        q_quantize(1)
+        q_quantize(1, 1)
+        q_product(4)
         value_squares(0)
+        q_transpose(2)
+        q_interleave(2)
+        q_transpose(3)
         value_squares(1)
+        q_interleave(3)
+        for c in range(C):
+            v_interleave(c)
+        value_times()
 
         for i in range(T):
-            distance(i)
+            if i == 0:
+                distance_part(0, 1)
+            else:
+                distance(i)
             if i + 1 < T:
                 scores(i + 1)
             if i == 0:
                 for c in range(C):
                     broadcast(g_row[:, c, :], g_b[:].rearrange("p c j -> p (c j)"), c)
-            if i >= 1:
-                inverse(i - 1)
+            if i >= 4 and i % 2 == 0:
+                time_copy(i // 2 - 2)
+                time_total(i // 2 - 2)
             if i >= 3:
                 pg_interleave(i - 3)
-            if i > 0 and i % 2 == 0 and i // 2 + 1 < T // 2:
-                q_interleave(i // 2 + 1)
-            if i >= 2:
-                time_sum(i - 2)
-            if i >= 4:
+            for p in range(4, 8):
+                if i == (2 * p - 4 if p % 2 == 0 else 2 * p - 5):
+                    q_interleave(p)
+            if i >= 5 and i % 2 == 1:
+                square_sum(i - 5)
                 square_sum(i - 4)
-                root(i - 4)
-            if i >= 5:
+                root_square(i - 5)
+                root(i - 5)
+            if i >= 6 and i % 2 == 0:
+                finish(i - 6)
                 finish(i - 5)
+            for p in range(4, 8):
+                if i == (2 * p - 5 if p % 2 == 0 else 2 * p - 6):
+                    q_transpose(p)
+            if i >= 4 and i % 2 == 0:
+                time_scale(i // 2 - 2)
             if i >= 2:
                 weights(i - 2)
                 pg_transpose(i - 2)
-            if i % 2 == 1 and (i + 3) // 2 < T // 2:
-                q_transpose((i + 3) // 2)
+            if i == 3:
+                time_fold(0)
+            if i >= 3:
+                time_fold(i - 2)
             minimum(i)
+            if i == T - 1:
+                pg_interleave(T - 3)
             exponent(i)
-            if i == 0:
-                q_product(8)
-                v_interleave(0)
-                v_interleave(1)
-            if i == 1:
-                value_times()
-                time_product(0)
-            if 1 <= i < T - 2:
+            if i >= T - 2:
+                inverse(i)
+            if 2 <= i < T - 2:
                 time_product(i)
-            if 1 <= i < T - 8:
-                q_product(i + 8)
+            if i < T - 2:
+                inverse(i)
             if i == 1:
-                v_quantize(0)
-                v_quantize(1)
-            if i >= 3:
-                pg_quantize(i - 3)
-            if i > 0 and i % 2 == 0 and i // 2 + 1 < T // 2:
-                q_quantize(i // 2 + 1)
-            if i >= 3:
+                value_rows()
+                time_product(0)
+                time_product(1)
+            if i % 2 == 1 and 1 < i < 8:
+                q_product((i + 7) // 2)
+            if i in (1, 5, 9):
+                q_quantize((i + 3) // 2, 2)
+            if i in (2, 3):
+                v_quantize(i - 2)
+            if i >= 4 and i % 2 == 0:
+                pg_quantize(i - 4, 2)
+                aggregate(i - 4)
                 aggregate(i - 3)
 
         weights(T - 2)
-        pg_interleave(T - 3)
         pg_transpose(T - 2)
-        pg_quantize(T - 3)
-        aggregate(T - 3)
-        square_sum(T - 4)
-        root(T - 4)
-        time_vector(T - 2)
+        pg_quantize(T - 4, 2)
         pg_interleave(T - 2)
-        inverse(T - 1)
+        aggregate(T - 4, "S0", None)
+        aggregate(T - 3, "S1", None)
+        time_copy(T // 2 - 2)
+        time_vector(T - 2)
+        square_sum(T - 6)
+        square_sum(T - 5)
+        root_square(T - 6)
+        root(T - 6)
         weights(T - 1)
         pg_transpose(T - 1, "qT")
-        pg_quantize(T - 2)
-        aggregate(T - 2, "S0", None)
-        finish(T - 5)
-        square_sum(T - 3)
-        root(T - 3)
         pg_interleave(T - 1)
+        time_total(T // 2 - 2)
+        time_scale(T // 2 - 2)
+        root_square(T - 4)
+        square_sum(T - 4)
+        square_sum(T - 3)
+        root(T - 4)
         time_vector(T - 1)
-        pg_quantize(T - 1)
-        aggregate(T - 1, "S1", None)
+        root_square(T - 2)
+        pg_quantize(T - 2, 1)
+        pg_quantize(T - 1, 1)
+        finish(T - 6, on_vector=True)
+        finish(T - 5, on_vector=True)
+        aggregate(T - 2)
+        aggregate(T - 1)
         square_sum(T - 2)
-        root(T - 2)
-        finish(T - 4)
-        finish(T - 3, on_vector=True)
+        root(T - 2, 1)
         square_sum(T - 1)
-        root(T - 1)
+        root(T - 1, 1)
+        finish(T - 4, on_vector=True)
+        finish(T - 3)
         finish(T - 2, on_vector=True)
         finish(T - 1)

@@ -18,6 +18,9 @@ AX = mybir.AxisListType
 
 P = 128
 T = N // P
+FOLD = ()
+GAIN = ()
+DUPS = True
 C = M // 512
 
 
@@ -34,13 +37,13 @@ def tile_lorentzcentroidaggregation_kernel(tc, q_bytes, q_scale, qt, k, kt, v, g
         v_raw = keep.tile([P, C, 4, E], BF16, name="v_raw")
         qs = keep.tile([P, D], F32, name="qs")
         qt_b = keep.tile([P, T], BF16, name="qt_b")
-        kt_b = keep.tile([P, C, 4], BF16, name="kt_b")
+        kt_all = keep.tile([P, M], BF16, name="kt_all")
+        g_all = keep.tile([P, M], BF16, name="g_all")
         g_b = keep.tile([P, C, 4], BF16, name="g_b")
 
         q_view = q_bytes.rearrange("(p i) d -> p i d", i=T)
         k_view = k.rearrange("(c p j) d -> p c j d", c=C, j=4)
         v_view = v.rearrange("(c p j) e -> p c j e", c=C, j=4)
-        nc.scalar.dma_start(out=kt_b[:], in_=kt.rearrange("(c p j) -> p c j", c=C, j=4))
         nc.scalar.dma_start(out=g_b[:], in_=g.rearrange("(c p j) -> p c j", c=C, j=4))
         nc.scalar.dma_start(out=qt_b[:], in_=qt.rearrange("(p i) -> p i", i=T))
         nc.sync.dma_start(out=k_raw[:, 0, 0:2, :], in_=k_view[:, 0, 0:2, :])
@@ -49,6 +52,8 @@ def tile_lorentzcentroidaggregation_kernel(tc, q_bytes, q_scale, qt, k, kt, v, g
         nc.sync.dma_start(out=k_raw[:, 0, 2:4, :], in_=k_view[:, 0, 2:4, :])
         nc.sync.dma_start(out=q_raw[:, 2:8, :], in_=q_view[:, 2:8, :])
         nc.sync.dma_start(out=k_raw[:, 1, :, :], in_=k_view[:, 1, :, :])
+        nc.sync.dma_start(out=kt_all[:], in_=kt.partition_broadcast(P))
+        nc.sync.dma_start(out=g_all[:], in_=g.partition_broadcast(P))
         nc.sync.dma_start(out=v_raw[:, 0, :, :], in_=v_view[:, 0, :, :])
         nc.sync.dma_start(out=v_raw[:, 1, :, :], in_=v_view[:, 1, :, :])
         nc.sync.dma_start(out=q_raw[:, 8:16, :], in_=q_view[:, 8:16, :])
@@ -68,10 +73,8 @@ def tile_lorentzcentroidaggregation_kernel(tc, q_bytes, q_scale, qt, k, kt, v, g
         warm_o = keep.tile([P, 1], F32, name="warm_o")
         nc.scalar.activation(warm_o[:], warm[:], ACT.Exp)
 
-        spread = keep.tile([P, 2, P, 2], BF16, name="spread")
-        nc.vector.memset(spread[:], 0.0)
-        for e in range(2):
-            nc.vector.tensor_copy(out=spread[:, e, :, e], in_=ident[:])
+        ident_b = keep.tile([P, P], BF16, name="ident_b")
+        nc.vector.tensor_copy(out=ident_b[:], in_=ident[:])
 
         qs2 = keep.tile([P, 2, D], F32, name="qs2")
         for h in range(2):
@@ -87,7 +90,8 @@ def tile_lorentzcentroidaggregation_kernel(tc, q_bytes, q_scale, qt, k, kt, v, g
         v_scales = keep.tile([P, C, 512], U8, name="v_scales", align_bytes=64)
         q_codes = keep.tile([P, T, P], U32, name="q_codes", align_bytes=64)
         q_scales = keep.tile([P, T, P], U8, name="q_scales", align_bytes=64)
-        kt_row = keep.tile([P, C, 512], F32, name="kt_row")
+        kt_row = keep.tile([P, C, 512], BF16, name="kt_row")
+        g_sb = keep.tile([P, C, 512], BF16, name="g_sb")
         vt_row = keep.tile([P, C, 512], F32, name="vt_row")
         ss = keep.tile([P, 8], F32, name="ss")
         vt16 = keep.tile([P, 8], F32, name="vt16")
@@ -99,16 +103,26 @@ def tile_lorentzcentroidaggregation_kernel(tc, q_bytes, q_scale, qt, k, kt, v, g
         us2 = keep.tile([P, T], F32, name="us2")
         sm = keep.tile([P, 3, T], F32, name="sm")
 
-        def broadcast(dst, cols, c):
-            for u in range(2):
-                for e in range(2):
-                    nc.tensor.matmul(
-                        dst[:, 256 * u : 256 * u + 256],
-                        lhsT=cols[:, 4 * c + 2 * u + e : 4 * c + 2 * u + e + 1].to_broadcast([P, P]),
-                        rhs=spread[:, e, :, :].rearrange("p a b -> p (a b)"),
-                        start=(e == 0),
-                        stop=(e == 1),
-                    )
+        def kt_order():
+            nc.vector.tensor_copy(
+                out=kt_row[:].rearrange("p c m -> p (c m)").bitcast(F32).rearrange("p (c u m) -> p c u m", c=C, u=2),
+                in_=kt_all[:].bitcast(F32).rearrange("p (c m u) -> p c u m", c=C, u=2),
+            )
+
+        def g_order():
+            if GAIN:
+                nc.gpsimd.tensor_copy(
+                    out=g_sb[:].rearrange("p c m -> p (c m)").bitcast(F32).rearrange("p (c u m) -> p c u m", c=C, u=2),
+                    in_=g_all[:].bitcast(F32).rearrange("p (c m u) -> p c u m", c=C, u=2),
+                )
+            for c in range(C):
+                nc.tensor.matmul(
+                    g_row[:, c, :],
+                    lhsT=ident_b[:],
+                    rhs=g_all[:, 512 * c : 512 * c + 512].rearrange("p (m u e) -> p u m e", u=2, e=2),
+                    start=True,
+                    stop=True,
+                )
 
         qf = {}
         qT = {}
@@ -218,7 +232,8 @@ def tile_lorentzcentroidaggregation_kernel(tc, q_bytes, q_scale, qt, k, kt, v, g
         S, y, ex, w, pg, pT, pgT, pcodes, pscales, us = {}, {}, {}, {}, {}, {}, {}, {}, {}, {}
 
         def scores_part(i, c):
-            S[i, c] = psum.tile([P, 512], F32, name="S", tag="S%d" % c)
+            if (i, c) not in S:
+                S[i, c] = psum.tile([P, 512], F32, name="S", tag="S%d" % c)
             nc.tensor.matmul_mx(
                 out=S[i, c][:],
                 lhsT=q_codes[:, i, :].bitcast(FP8X4),
@@ -266,7 +281,10 @@ def tile_lorentzcentroidaggregation_kernel(tc, q_bytes, q_scale, qt, k, kt, v, g
             )
 
         def inverse(i):
-            nc.gpsimd.tensor_tensor(out=rinv[:, i : i + 1], in0=rsum[:, i : i + 1], in1=minus1[:], op=ALU.pow)
+            if i == T - 1:
+                nc.vector.reciprocal(out=rinv[:, i : i + 1], in_=rsum[:, i : i + 1])
+            else:
+                nc.gpsimd.tensor_tensor(out=rinv[:, i : i + 1], in0=rsum[:, i : i + 1], in1=minus1[:], op=ALU.pow)
 
         def weights(i):
             pg[i] = work.tile([P, C, 512], BF16, name="pg", tag="pg")
@@ -279,12 +297,28 @@ def tile_lorentzcentroidaggregation_kernel(tc, q_bytes, q_scale, qt, k, kt, v, g
                 op1=ALU.mult,
             )
 
+        eg = {}
+
+        def gain_product(i, c):
+            if c == 0:
+                eg[i] = work.tile([P, C, 512], F32, name="eg", tag="eg", bufs=2)
+            nc.gpsimd.tensor_tensor(out=eg[i][:, c, :], in0=ex[i][:, c, :], in1=g_sb[:, c, :], op=ALU.mult)
+
+        def weights_scalar(i):
+            pg[i] = work.tile([P, C, 512], BF16, name="pg", tag="pg")
+            nc.scalar.activation(
+                pg[i][:].rearrange("p c m -> p (c m)"),
+                eg[i][:].rearrange("p c m -> p (c m)"),
+                ACT.Copy,
+                scale=rinv[:, i : i + 1],
+            )
+
         def time_product(i):
             w[i] = work.tile([P, C, 512], F32, name="w", tag="w", bufs=4)
             nc.gpsimd.tensor_tensor(out=w[i][:], in0=ex[i][:], in1=vt_row[:], op=ALU.mult)
 
         def time_vector(i):
-            junk = work.tile([P, C, 512], BF16, name="junk_w", tag="junk_w", bufs=1)
+            junk = work.tile([P, C, 512], BF16, name="junk_w", tag="junk_w", bufs=2)
             nc.vector.scalar_tensor_tensor(
                 out=junk[:].rearrange("p c m -> p (c m)"),
                 in0=ex[i][:].rearrange("p c m -> p (c m)"),
@@ -292,6 +326,16 @@ def tile_lorentzcentroidaggregation_kernel(tc, q_bytes, q_scale, qt, k, kt, v, g
                 in1=vt_row[:].rearrange("p c m -> p (c m)"),
                 op0=ALU.mult,
                 op1=ALU.mult,
+                accum_out=ut[:, i : i + 1],
+            )
+
+        def time_sum(i):
+            junk = work.tile([P, C, 512], BF16, name="junk_t", tag="junk_w", bufs=2)
+            nc.scalar.activation(
+                junk[:].rearrange("p c m -> p (c m)"),
+                w[i][:].rearrange("p c m -> p (c m)"),
+                ACT.Copy,
+                scale=rinv[:, i : i + 1],
                 accum_out=ut[:, i : i + 1],
             )
 
@@ -355,6 +399,9 @@ def tile_lorentzcentroidaggregation_kernel(tc, q_bytes, q_scale, qt, k, kt, v, g
 
         def aggregate(i, tag="us", bufs=2):
             us[i] = psum.tile([P, E], F32, name="us", tag=tag, bufs=bufs)
+            aggregate_again(i)
+
+        def aggregate_again(i):
             for c in range(C):
                 nc.tensor.matmul_mx(
                     out=us[i][:],
@@ -389,10 +436,6 @@ def tile_lorentzcentroidaggregation_kernel(tc, q_bytes, q_scale, qt, k, kt, v, g
                 nc.scalar.activation(o[:], us[i][:], ACT.Copy, scale=sm[:, 2, i : i + 1])
             nc.sync.dma_start(out=out_view[:, i, :], in_=o[:])
 
-        kt_ps = {}
-        for c in range(C):
-            kt_ps[c] = psum.tile([P, 512], F32, name="kt_ps", tag="S%d" % c)
-            broadcast(kt_ps[c], kt_b[:].rearrange("p c j -> p (c j)"), c)
         k_transpose(0, 0, "us", 2)
         k_interleave(0, 0, nc.scalar.copy)
         q_product(0)
@@ -403,10 +446,9 @@ def tile_lorentzcentroidaggregation_kernel(tc, q_bytes, q_scale, qt, k, kt, v, g
         k_transpose(1, 0, "pT", None)
         k_interleave(1, 0, nc.scalar.copy)
         q_product(1)
-        for c in range(C):
-            nc.scalar.copy(out=kt_row[:, c, :], in_=kt_ps[c][:])
         k_transpose(1, 1, "us", 2)
         k_interleave(1, 1, nc.scalar.copy)
+        kt_order()
         q_product(2)
         k_quantize(0)
         q_quantize(0, 1)
@@ -436,51 +478,64 @@ def tile_lorentzcentroidaggregation_kernel(tc, q_bytes, q_scale, qt, k, kt, v, g
                 distance(i)
             if i + 1 < T:
                 scores(i + 1)
+                if DUPS and i % 2 == 1:
+                    scores(i + 1)
             if i == 0:
-                for c in range(C):
-                    broadcast(g_row[:, c, :], g_b[:].rearrange("p c j -> p (c j)"), c)
-            if i >= 4 and i % 2 == 0:
-                time_copy(i // 2 - 2)
-                time_total(i // 2 - 2)
+                g_order()
+            pair = i // 2 - 2
+            if i >= 4 and i % 2 == 0 and pair in FOLD:
+                time_copy(pair)
+                time_total(pair)
             if i >= 3:
                 pg_interleave(i - 3)
-            for p in range(4, 8):
-                if i == (2 * p - 4 if p % 2 == 0 else 2 * p - 5):
-                    q_interleave(p)
-            if i >= 5 and i % 2 == 1:
+            if 5 <= i < T - 1 and i % 2 == 1:
                 square_sum(i - 5)
                 square_sum(i - 4)
-                root_square(i - 5)
                 root(i - 5)
             if i >= 6 and i % 2 == 0:
                 finish(i - 6)
                 finish(i - 5)
             for p in range(4, 8):
+                if i == (2 * p - 4 if p % 2 == 0 else 2 * p - 5):
+                    q_interleave(p)
+            for p in range(4, 8):
                 if i == (2 * p - 5 if p % 2 == 0 else 2 * p - 6):
                     q_transpose(p)
-            if i >= 4 and i % 2 == 0:
-                time_scale(i // 2 - 2)
+            if i >= 4 and i % 2 == 0 and pair in FOLD:
+                time_scale(pair)
+            if i >= 3 and (i - 3) // 2 not in FOLD:
+                time_sum(i - 3)
             if i >= 2:
-                weights(i - 2)
+                if i - 2 in GAIN:
+                    weights_scalar(i - 2)
+                else:
+                    weights(i - 2)
                 pg_transpose(i - 2)
-            if i == 3:
+            if DUPS and i % 2 == 0 and 2 <= i and i + 1 < T:
+                scores(i + 1)
+            if i >= 4 and i % 2 == 0:
+                root_square(i - 4)
+            if i == 3 and 0 in FOLD:
                 time_fold(0)
-            if i >= 3:
+            if i >= 3 and (i - 2) // 2 in FOLD:
                 time_fold(i - 2)
             minimum(i)
             if i == T - 1:
-                pg_interleave(T - 3)
+                square_sum(T - 6)
             exponent(i)
-            if i >= T - 2:
-                inverse(i)
-            if 2 <= i < T - 2:
-                time_product(i)
-            if i < T - 2:
+            if i < 2 or i == T - 2:
                 inverse(i)
             if i == 1:
                 value_rows()
                 time_product(0)
                 time_product(1)
+            if 2 <= i < T - 2:
+                if i < T - 3:
+                    time_product(i)
+                inverse(i)
+                if i in GAIN:
+                    for c in range(C):
+                        gain_product(i, c)
             if i % 2 == 1 and 1 < i < 8:
                 q_product((i + 7) // 2)
             if i in (1, 5, 9):
@@ -491,40 +546,40 @@ def tile_lorentzcentroidaggregation_kernel(tc, q_bytes, q_scale, qt, k, kt, v, g
                 pg_quantize(i - 4, 2)
                 aggregate(i - 4)
                 aggregate(i - 3)
+            if i >= 5 and i % 2 == 1:
+                if DUPS:
+                    aggregate_again(i - 4)
 
         weights(T - 2)
         pg_transpose(T - 2)
-        pg_quantize(T - 4, 2)
+        pg_interleave(T - 3)
         pg_interleave(T - 2)
-        aggregate(T - 4, "S0", None)
-        aggregate(T - 3, "S1", None)
-        time_copy(T // 2 - 2)
-        time_vector(T - 2)
-        square_sum(T - 6)
-        square_sum(T - 5)
-        root_square(T - 6)
-        root(T - 6)
+        time_vector(T - 3)
+        inverse(T - 1)
+        root_square(T - 4)
         weights(T - 1)
         pg_transpose(T - 1, "qT")
+        pg_quantize(T - 4, 2)
+        aggregate(T - 4, "S0", None)
+        aggregate(T - 3, "S1", None)
+        square_sum(T - 5)
+        root(T - 6)
+        pg_quantize(T - 2, 1)
+        aggregate(T - 2)
         pg_interleave(T - 1)
-        time_total(T // 2 - 2)
-        time_scale(T // 2 - 2)
-        root_square(T - 4)
+        time_vector(T - 2)
+        pg_quantize(T - 1, 1)
+        aggregate(T - 1)
+        time_vector(T - 1)
+        root_square(T - 2)
         square_sum(T - 4)
         square_sum(T - 3)
         root(T - 4)
-        time_vector(T - 1)
-        root_square(T - 2)
-        pg_quantize(T - 2, 1)
-        pg_quantize(T - 1, 1)
         finish(T - 6, on_vector=True)
         finish(T - 5, on_vector=True)
-        aggregate(T - 2)
-        aggregate(T - 1)
         square_sum(T - 2)
-        root(T - 2, 1)
         square_sum(T - 1)
-        root(T - 1, 1)
+        root(T - 2)
         finish(T - 4, on_vector=True)
         finish(T - 3)
         finish(T - 2, on_vector=True)

@@ -18,9 +18,10 @@ AX = mybir.AxisListType
 
 P = 128
 T = N // P
-FOLD = ()
-GAIN = ()
-DUPS = True
+UT_V = (13, 14, 15)
+Q_STEP = {4: 2, 5: 3, 6: 5, 7: 7}
+QP_STEP = {5: 2, 6: 4, 7: 6}
+QQ_STEP = {2: 1, 4: 5, 6: 8}
 C = M // 512
 
 
@@ -35,25 +36,23 @@ def tile_lorentzcentroidaggregation_kernel(tc, q_bytes, q_scale, qt, k, kt, v, g
         q_raw = keep.tile([P, T, D], U8, name="q_raw")
         k_raw = keep.tile([P, C, 4, D], BF16, name="k_raw")
         v_raw = keep.tile([P, C, 4, E], BF16, name="v_raw")
-        qs = keep.tile([P, D], F32, name="qs")
+        qs_c = keep.tile([P, 4], F32, name="qs_c")
         qt_b = keep.tile([P, T], BF16, name="qt_b")
-        kt_all = keep.tile([P, M], BF16, name="kt_all")
-        g_all = keep.tile([P, M], BF16, name="g_all")
+        kt_b = keep.tile([P, C, 4], BF16, name="kt_b")
         g_b = keep.tile([P, C, 4], BF16, name="g_b")
 
         q_view = q_bytes.rearrange("(p i) d -> p i d", i=T)
         k_view = k.rearrange("(c p j) d -> p c j d", c=C, j=4)
         v_view = v.rearrange("(c p j) e -> p c j e", c=C, j=4)
+        nc.scalar.dma_start(out=qs_c[:], in_=q_scale.rearrange("o (p j) -> p (o j)", j=4))
+        nc.scalar.dma_start(out=kt_b[:], in_=kt.rearrange("(c p j) -> p c j", c=C, j=4))
         nc.scalar.dma_start(out=g_b[:], in_=g.rearrange("(c p j) -> p c j", c=C, j=4))
         nc.scalar.dma_start(out=qt_b[:], in_=qt.rearrange("(p i) -> p i", i=T))
         nc.sync.dma_start(out=k_raw[:, 0, 0:2, :], in_=k_view[:, 0, 0:2, :])
-        nc.sync.dma_start(out=qs[:], in_=q_scale.rearrange("o d -> (o d)").partition_broadcast(P))
         nc.sync.dma_start(out=q_raw[:, 0:2, :], in_=q_view[:, 0:2, :])
         nc.sync.dma_start(out=k_raw[:, 0, 2:4, :], in_=k_view[:, 0, 2:4, :])
         nc.sync.dma_start(out=q_raw[:, 2:8, :], in_=q_view[:, 2:8, :])
         nc.sync.dma_start(out=k_raw[:, 1, :, :], in_=k_view[:, 1, :, :])
-        nc.sync.dma_start(out=kt_all[:], in_=kt.partition_broadcast(P))
-        nc.sync.dma_start(out=g_all[:], in_=g.partition_broadcast(P))
         nc.sync.dma_start(out=v_raw[:, 0, :, :], in_=v_view[:, 0, :, :])
         nc.sync.dma_start(out=v_raw[:, 1, :, :], in_=v_view[:, 1, :, :])
         nc.sync.dma_start(out=q_raw[:, 8:16, :], in_=q_view[:, 8:16, :])
@@ -62,10 +61,6 @@ def tile_lorentzcentroidaggregation_kernel(tc, q_bytes, q_scale, qt, k, kt, v, g
         make_identity(nc, ident[:])
         half = keep.tile([P, 8], F32, name="half")
         nhalf = keep.tile([P, 2], F32, name="nhalf")
-        minus1 = keep.tile([P, 1], F32, name="minus1")
-        ones = keep.tile([P, 1], F32, name="ones")
-        nc.gpsimd.memset(minus1[:], -1.0)
-        nc.gpsimd.memset(ones[:], 1.0)
         nc.gpsimd.memset(half[:], 0.5)
         nc.gpsimd.memset(nhalf[:], -0.5)
         warm = keep.tile([P, 1], F32, name="warm")
@@ -73,12 +68,25 @@ def tile_lorentzcentroidaggregation_kernel(tc, q_bytes, q_scale, qt, k, kt, v, g
         warm_o = keep.tile([P, 1], F32, name="warm_o")
         nc.scalar.activation(warm_o[:], warm[:], ACT.Exp)
 
-        ident_b = keep.tile([P, P], BF16, name="ident_b")
-        nc.vector.tensor_copy(out=ident_b[:], in_=ident[:])
+        spread = keep.tile([P, 2, P, 2], BF16, name="spread")
+        nc.vector.memset(spread[:], 0.0)
+        for e in range(2):
+            nc.vector.tensor_copy(out=spread[:, e, :, e], in_=ident[:])
 
         qs2 = keep.tile([P, 2, D], F32, name="qs2")
-        for h in range(2):
-            nc.vector.tensor_scalar(out=qs2[:, h, :], in0=qs[:], scalar1=2.0, scalar2=None, op0=ALU.mult)
+        qs_ps = psum.tile([P, 4, P], F32, name="qs_ps", tag="pT")
+        for j in range(4):
+            nc.tensor.transpose(qs_ps[:, j, :], qs_c[:, j : j + 1].to_broadcast([P, P]), ident[:])
+        nc.vector.tensor_scalar(
+            out=qs2[:, 0, :].rearrange("p (d j) -> p d j", j=4),
+            in0=qs_ps[:].rearrange("p j d -> p d j"),
+            scalar1=2.0,
+            scalar2=None,
+            op0=ALU.mult,
+        )
+        nc.vector.tensor_copy(out=qs2[:, 1, :], in_=qs2[:, 0, :])
+        kt_f = keep.tile([P, 8], F32, name="kt_f")
+        nc.vector.tensor_copy(out=kt_f[:], in_=kt_b[:].rearrange("p c j -> p (c j)"))
         qt2 = keep.tile([P, T], F32, name="qt2")
         nc.vector.tensor_scalar(out=qt2[:], in0=qt_b[:], scalar1=2.0, scalar2=None, op0=ALU.mult)
         g_f = keep.tile([P, 8], F32, name="g_f")
@@ -91,7 +99,6 @@ def tile_lorentzcentroidaggregation_kernel(tc, q_bytes, q_scale, qt, k, kt, v, g
         q_codes = keep.tile([P, T, P], U32, name="q_codes", align_bytes=64)
         q_scales = keep.tile([P, T, P], U8, name="q_scales", align_bytes=64)
         kt_row = keep.tile([P, C, 512], BF16, name="kt_row")
-        g_sb = keep.tile([P, C, 512], BF16, name="g_sb")
         vt_row = keep.tile([P, C, 512], F32, name="vt_row")
         ss = keep.tile([P, 8], F32, name="ss")
         vt16 = keep.tile([P, 8], F32, name="vt16")
@@ -103,26 +110,28 @@ def tile_lorentzcentroidaggregation_kernel(tc, q_bytes, q_scale, qt, k, kt, v, g
         us2 = keep.tile([P, T], F32, name="us2")
         sm = keep.tile([P, 3, T], F32, name="sm")
 
-        def kt_order():
-            nc.vector.tensor_copy(
-                out=kt_row[:].rearrange("p c m -> p (c m)").bitcast(F32).rearrange("p (c u m) -> p c u m", c=C, u=2),
-                in_=kt_all[:].bitcast(F32).rearrange("p (c m u) -> p c u m", c=C, u=2),
+        def row_of(cols, c, tag, bufs, out, copy):
+            ps = psum.tile([P, 2, 2, P], F32, name="row_ps", tag=tag, bufs=bufs)
+            for u in range(2):
+                for e in range(2):
+                    n = 4 * c + 2 * u + e
+                    nc.tensor.transpose(ps[:, u, e, :], cols[:, n : n + 1].to_broadcast([P, P]), ident[:])
+            copy(
+                out=out[:, c, :].rearrange("p (u m e) -> p u m e", u=2, e=2),
+                in_=ps[:].rearrange("p u e m -> p u m e"),
             )
 
         def g_order():
-            if GAIN:
-                nc.gpsimd.tensor_copy(
-                    out=g_sb[:].rearrange("p c m -> p (c m)").bitcast(F32).rearrange("p (c u m) -> p c u m", c=C, u=2),
-                    in_=g_all[:].bitcast(F32).rearrange("p (c m u) -> p c u m", c=C, u=2),
-                )
             for c in range(C):
-                nc.tensor.matmul(
-                    g_row[:, c, :],
-                    lhsT=ident_b[:],
-                    rhs=g_all[:, 512 * c : 512 * c + 512].rearrange("p (m u e) -> p u m e", u=2, e=2),
-                    start=True,
-                    stop=True,
-                )
+                for u in range(2):
+                    for e in range(2):
+                        nc.tensor.matmul(
+                            g_row[:, c, 256 * u : 256 * u + 256],
+                            lhsT=g_b[:, c, 2 * u + e : 2 * u + e + 1].to_broadcast([P, P]),
+                            rhs=spread[:, e, :, :].rearrange("p m e -> p (m e)"),
+                            start=(e == 0),
+                            stop=(e == 1),
+                        )
 
         qf = {}
         qT = {}
@@ -199,15 +208,7 @@ def tile_lorentzcentroidaggregation_kernel(tc, q_bytes, q_scale, qt, k, kt, v, g
 
         def value_rows():
             for c in range(C):
-                vt_ps = psum.tile([P, 2, 2, P], F32, name="vt_ps", tag="us", bufs=2)
-                for u in range(2):
-                    for e in range(2):
-                        n = 4 * c + 2 * u + e
-                        nc.tensor.transpose(vt_ps[:, u, e, :], vt16[:, n : n + 1].to_broadcast([P, P]), ident[:])
-                nc.scalar.copy(
-                    out=vt_row[:, c, :].rearrange("p (u m e) -> p u m e", u=2, e=2),
-                    in_=vt_ps[:].rearrange("p u e m -> p u m e"),
-                )
+                row_of(vt16, c, "us", 3, vt_row, nc.scalar.copy)
 
         def v_interleave(c):
             vg[c] = work.tile([P, E, 4], BF16, name="vg", tag="vg", align_bytes=64)
@@ -281,10 +282,7 @@ def tile_lorentzcentroidaggregation_kernel(tc, q_bytes, q_scale, qt, k, kt, v, g
             )
 
         def inverse(i):
-            if i == T - 1:
-                nc.vector.reciprocal(out=rinv[:, i : i + 1], in_=rsum[:, i : i + 1])
-            else:
-                nc.gpsimd.tensor_tensor(out=rinv[:, i : i + 1], in0=rsum[:, i : i + 1], in1=minus1[:], op=ALU.pow)
+            nc.vector.reciprocal(out=rinv[:, i : i + 1], in_=rsum[:, i : i + 1])
 
         def weights(i):
             pg[i] = work.tile([P, C, 512], BF16, name="pg", tag="pg")
@@ -295,22 +293,6 @@ def tile_lorentzcentroidaggregation_kernel(tc, q_bytes, q_scale, qt, k, kt, v, g
                 in1=g_row[:].rearrange("p c m -> p (c m)"),
                 op0=ALU.mult,
                 op1=ALU.mult,
-            )
-
-        eg = {}
-
-        def gain_product(i, c):
-            if c == 0:
-                eg[i] = work.tile([P, C, 512], F32, name="eg", tag="eg", bufs=2)
-            nc.gpsimd.tensor_tensor(out=eg[i][:, c, :], in0=ex[i][:, c, :], in1=g_sb[:, c, :], op=ALU.mult)
-
-        def weights_scalar(i):
-            pg[i] = work.tile([P, C, 512], BF16, name="pg", tag="pg")
-            nc.scalar.activation(
-                pg[i][:].rearrange("p c m -> p (c m)"),
-                eg[i][:].rearrange("p c m -> p (c m)"),
-                ACT.Copy,
-                scale=rinv[:, i : i + 1],
             )
 
         def time_product(i):
@@ -339,37 +321,6 @@ def tile_lorentzcentroidaggregation_kernel(tc, q_bytes, q_scale, qt, k, kt, v, g
                 accum_out=ut[:, i : i + 1],
             )
 
-        wT, ws = {}, {}
-
-        def time_fold(i):
-            if i % 2 == 0:
-                wT[i // 2] = psum.tile([P, 3, P], F32, name="wT", tag="wT")
-            flat = w[i][:].rearrange("p c m -> p (c m)")
-            for b in range(8):
-                nc.tensor.matmul(
-                    wT[i // 2][:, i % 2, :],
-                    lhsT=flat[:, P * b : P * b + P],
-                    rhs=ident[:],
-                    is_transpose=True,
-                    start=(b == 0),
-                    stop=(b == 7),
-                )
-
-        def time_copy(pair):
-            ws[pair] = work.tile([P, 2, P], F32, name="ws", tag="ws")
-            nc.scalar.copy(out=ws[pair][:], in_=wT[pair][:, 0:2, :])
-
-        def time_total(pair):
-            for h in range(2):
-                nc.tensor.matmul(
-                    wT[pair][:, 2, h : h + 1], lhsT=ws[pair][:, h, :], rhs=ones[:], start=True, stop=True
-                )
-
-        def time_scale(pair):
-            for h in range(2):
-                i = 2 * pair + h
-                nc.scalar.activation(ut[:, i : i + 1], wT[pair][:, 2, h : h + 1], ACT.Copy, scale=rinv[:, i : i + 1])
-
         def pg_transpose(i, tag="pT"):
             pT[i] = psum.tile([P, C, 2, P], F32, name="pT", tag=tag)
             words = pg[i][:].rearrange("p c m -> p (c m)").bitcast(F32)
@@ -397,7 +348,7 @@ def tile_lorentzcentroidaggregation_kernel(tc, q_bytes, q_scale, qt, k, kt, v, g
                 in_=pgT[i // 2][:, part, :].rearrange("p i x -> p (i x)"),
             )
 
-        def aggregate(i, tag="us", bufs=2):
+        def aggregate(i, tag="us", bufs=3):
             us[i] = psum.tile([P, E], F32, name="us", tag=tag, bufs=bufs)
             aggregate_again(i)
 
@@ -429,26 +380,27 @@ def tile_lorentzcentroidaggregation_kernel(tc, q_bytes, q_scale, qt, k, kt, v, g
         out_view = out.rearrange("(p i) e -> p i e", i=T)
 
         def finish(i, on_vector=False):
-            o = work.tile([P, E], F32, name="o", tag="o", bufs=3)
+            o = work.tile([P, E], F32, name="o", tag="o", bufs=6)
             if on_vector:
                 nc.vector.tensor_scalar(out=o[:], in0=us[i][:], scalar1=sm[:, 2, i : i + 1], scalar2=None, op0=ALU.mult)
             else:
                 nc.scalar.activation(o[:], us[i][:], ACT.Copy, scale=sm[:, 2, i : i + 1])
             nc.sync.dma_start(out=out_view[:, i, :], in_=o[:])
 
-        k_transpose(0, 0, "us", 2)
+        k_transpose(0, 0, "us", 3)
         k_interleave(0, 0, nc.scalar.copy)
         q_product(0)
-        k_transpose(0, 1, "us", 2)
+        k_transpose(0, 1, "us", 3)
         k_interleave(0, 1, nc.scalar.copy)
         q_transpose(0)
         q_interleave(0)
         k_transpose(1, 0, "pT", None)
         k_interleave(1, 0, nc.scalar.copy)
         q_product(1)
-        k_transpose(1, 1, "us", 2)
+        k_transpose(1, 1, "us", 3)
         k_interleave(1, 1, nc.scalar.copy)
-        kt_order()
+        for c in range(C):
+            row_of(kt_f, c, "S%d" % c, None, kt_row, nc.scalar.copy)
         q_product(2)
         k_quantize(0)
         q_quantize(0, 1)
@@ -464,123 +416,110 @@ def tile_lorentzcentroidaggregation_kernel(tc, q_bytes, q_scale, qt, k, kt, v, g
         value_squares(0)
         q_transpose(2)
         q_interleave(2)
-        q_transpose(3)
         value_squares(1)
-        q_interleave(3)
         for c in range(C):
             v_interleave(c)
         value_times()
 
         for i in range(T):
+            last = i == T - 1
+            if i >= 2:
+                inverse(i - 2)
             if i == 0:
                 distance_part(0, 1)
             else:
                 distance(i)
-            if i + 1 < T:
+            if not last:
                 scores(i + 1)
-                if DUPS and i % 2 == 1:
-                    scores(i + 1)
+                if i >= 1:
+                    scores_part(i + 1, 1)
+            else:
+                aggregate(i - 4, "S0", None)
             if i == 0:
+                q_transpose(3)
                 g_order()
-            pair = i // 2 - 2
-            if i >= 4 and i % 2 == 0 and pair in FOLD:
-                time_copy(pair)
-                time_total(pair)
             if i >= 3:
                 pg_interleave(i - 3)
-            if 5 <= i < T - 1 and i % 2 == 1:
+                time_sum(i - 3)
+            if i >= 5:
                 square_sum(i - 5)
-                square_sum(i - 4)
-                root(i - 5)
             if i >= 6 and i % 2 == 0:
+                root(i - 6)
+            if i >= 7 and i % 2 == 1 and not last:
+                finish(i - 7)
                 finish(i - 6)
-                finish(i - 5)
             for p in range(4, 8):
-                if i == (2 * p - 4 if p % 2 == 0 else 2 * p - 5):
+                if i == Q_STEP[p] + 1:
                     q_interleave(p)
             for p in range(4, 8):
-                if i == (2 * p - 5 if p % 2 == 0 else 2 * p - 6):
+                if i == Q_STEP[p]:
                     q_transpose(p)
-            if i >= 4 and i % 2 == 0 and pair in FOLD:
-                time_scale(pair)
-            if i >= 3 and (i - 3) // 2 not in FOLD:
-                time_sum(i - 3)
             if i >= 2:
-                if i - 2 in GAIN:
-                    weights_scalar(i - 2)
-                else:
-                    weights(i - 2)
+                weights(i - 2)
                 pg_transpose(i - 2)
-            if DUPS and i % 2 == 0 and 2 <= i and i + 1 < T:
-                scores(i + 1)
             if i >= 4 and i % 2 == 0:
                 root_square(i - 4)
-            if i == 3 and 0 in FOLD:
-                time_fold(0)
-            if i >= 3 and (i - 2) // 2 in FOLD:
-                time_fold(i - 2)
+            if last:
+                inverse(T - 2)
             minimum(i)
-            if i == T - 1:
-                square_sum(T - 6)
             exponent(i)
-            if i < 2 or i == T - 2:
-                inverse(i)
+            if i == 0:
+                q_interleave(3)
             if i == 1:
                 value_rows()
                 time_product(0)
                 time_product(1)
             if 2 <= i < T - 2:
-                if i < T - 3:
+                if i not in UT_V:
                     time_product(i)
-                inverse(i)
-                if i in GAIN:
-                    for c in range(C):
-                        gain_product(i, c)
-            if i % 2 == 1 and 1 < i < 8:
-                q_product((i + 7) // 2)
-            if i in (1, 5, 9):
-                q_quantize((i + 3) // 2, 2)
+            for p in range(5, 8):
+                if i == QP_STEP[p]:
+                    q_product(p)
+            for p in (2, 4, 6):
+                if i == QQ_STEP[p]:
+                    q_quantize(p, 2)
             if i in (2, 3):
                 v_quantize(i - 2)
             if i >= 4 and i % 2 == 0:
                 pg_quantize(i - 4, 2)
                 aggregate(i - 4)
-                aggregate(i - 3)
-            if i >= 5 and i % 2 == 1:
-                if DUPS:
-                    aggregate_again(i - 4)
+            if i >= 5 and i % 2 == 1 and not last:
+                aggregate(i - 4)
 
         weights(T - 2)
-        pg_transpose(T - 2)
+        pg_transpose(T - 2, "qT")
+        pg_quantize(T - 4, 1)
+        aggregate(T - 4, "S1", None)
         pg_interleave(T - 3)
-        pg_interleave(T - 2)
         time_vector(T - 3)
+        pg_interleave(T - 2)
+        finish(T - 8)
+        finish(T - 7)
         inverse(T - 1)
         root_square(T - 4)
         weights(T - 1)
-        pg_transpose(T - 1, "qT")
-        pg_quantize(T - 4, 2)
-        aggregate(T - 4, "S0", None)
-        aggregate(T - 3, "S1", None)
-        square_sum(T - 5)
-        root(T - 6)
+        pg_transpose(T - 1)
+        pg_quantize(T - 3, 1)
+        aggregate(T - 3)
         pg_quantize(T - 2, 1)
         aggregate(T - 2)
+        square_sum(T - 5)
+        root(T - 6)
         pg_interleave(T - 1)
         time_vector(T - 2)
         pg_quantize(T - 1, 1)
-        aggregate(T - 1)
+        aggregate(T - 1, "qT", None)
         time_vector(T - 1)
-        root_square(T - 2)
         square_sum(T - 4)
         square_sum(T - 3)
         root(T - 4)
+        root_square(T - 2)
         finish(T - 6, on_vector=True)
-        finish(T - 5, on_vector=True)
         square_sum(T - 2)
         square_sum(T - 1)
         root(T - 2)
-        finish(T - 4, on_vector=True)
-        finish(T - 3)
-        finish(T - 2, on_vector=True)
-        finish(T - 1)
+        finish(T - 5, on_vector=True)
+        finish(T - 4)
+        finish(T - 3, on_vector=True)
+        finish(T - 2)
+        finish(T - 1, on_vector=True)

from contextlib import ExitStack

import concourse.mybir as mybir
from concourse.masks import make_identity

N, M, D, E = 2048, 1024, 512, 512
FLOPS = 2 * N * M * D + 2 * N * M * E

F32 = mybir.dt.float32
BF16 = mybir.dt.bfloat16
U32 = mybir.dt.uint32
U8 = mybir.dt.uint8
FP8 = mybir.dt.float8_e4m3fn
FP8X4 = mybir.dt.float8_e4m3fn_x4
ALU = mybir.AluOpType
ACT = mybir.ActivationFunctionType
AX = mybir.AxisListType

P = 128
T = N // P
UT_V = (13, 14, 15)
Q_STEP = {4: 2, 5: 3, 6: 5, 7: 7}
QP_STEP = {5: 2, 6: 4, 7: 6}
QQ_STEP = {2: 1, 4: 5, 6: 8}
C = M // 512


def tile_lorentzcentroidaggregation_kernel(tc, q_bytes, q_scale, qt, k, kt, v, g, out):
    nc = tc.nc
    with ExitStack() as ctx:
        keep = ctx.enter_context(tc.tile_pool(name="keep", bufs=1))
        work = ctx.enter_context(tc.tile_pool(name="work", bufs=2))
        psum = ctx.enter_context(tc.psum_pool(name="psum", bufs=1))
        ctx.enter_context(tc.manual_schedule())

        q_raw = keep.tile([P, T, D], U8, name="q_raw")
        k_raw = keep.tile([P, C, 4, D], BF16, name="k_raw")
        v_raw = keep.tile([P, C, 4, E], BF16, name="v_raw")
        qs_c = keep.tile([P, 4], F32, name="qs_c")
        qt_b = keep.tile([P, T], BF16, name="qt_b")
        kt_b = keep.tile([P, C, 4], BF16, name="kt_b")
        g_b = keep.tile([P, C, 4], BF16, name="g_b")

        q_view = q_bytes.rearrange("(p i) d -> p i d", i=T)
        k_view = k.rearrange("(c p j) d -> p c j d", c=C, j=4)
        v_view = v.rearrange("(c p j) e -> p c j e", c=C, j=4)
        nc.scalar.dma_start(out=qs_c[:], in_=q_scale.rearrange("o (p j) -> p (o j)", j=4))
        nc.scalar.dma_start(out=kt_b[:], in_=kt.rearrange("(c p j) -> p c j", c=C, j=4))
        nc.scalar.dma_start(out=g_b[:], in_=g.rearrange("(c p j) -> p c j", c=C, j=4))
        nc.scalar.dma_start(out=qt_b[:], in_=qt.rearrange("(p i) -> p i", i=T))
        nc.sync.dma_start(out=k_raw[:, 0, 0:2, :], in_=k_view[:, 0, 0:2, :])
        nc.sync.dma_start(out=q_raw[:, 0:2, :], in_=q_view[:, 0:2, :])
        nc.sync.dma_start(out=k_raw[:, 0, 2:4, :], in_=k_view[:, 0, 2:4, :])
        nc.sync.dma_start(out=q_raw[:, 2:8, :], in_=q_view[:, 2:8, :])
        nc.sync.dma_start(out=k_raw[:, 1, :, :], in_=k_view[:, 1, :, :])
        nc.sync.dma_start(out=v_raw[:, 0, :, :], in_=v_view[:, 0, :, :])
        nc.sync.dma_start(out=v_raw[:, 1, :, :], in_=v_view[:, 1, :, :])
        nc.sync.dma_start(out=q_raw[:, 8:16, :], in_=q_view[:, 8:16, :])

        ident = keep.tile([P, P], F32, name="ident")
        make_identity(nc, ident[:])
        half = keep.tile([P, 8], F32, name="half")
        nhalf = keep.tile([P, 2], F32, name="nhalf")
        nc.gpsimd.memset(half[:], 0.5)
        nc.gpsimd.memset(nhalf[:], -0.5)
        warm = keep.tile([P, 1], F32, name="warm")
        nc.vector.memset(warm[:], 0.0)
        warm_o = keep.tile([P, 1], F32, name="warm_o")
        nc.scalar.activation(warm_o[:], warm[:], ACT.Exp)

        spread = keep.tile([P, 2, P, 2], BF16, name="spread")
        nc.vector.memset(spread[:], 0.0)
        for e in range(2):
            nc.vector.tensor_copy(out=spread[:, e, :, e], in_=ident[:])

        qs2 = keep.tile([P, 2, D], F32, name="qs2")
        qs_ps = psum.tile([P, 4, P], F32, name="qs_ps", tag="pT")
        for j in range(4):
            nc.tensor.transpose(qs_ps[:, j, :], qs_c[:, j : j + 1].to_broadcast([P, P]), ident[:])
        nc.vector.tensor_scalar(
            out=qs2[:, 0, :].rearrange("p (d j) -> p d j", j=4),
            in0=qs_ps[:].rearrange("p j d -> p d j"),
            scalar1=2.0,
            scalar2=None,
            op0=ALU.mult,
        )
        nc.vector.tensor_copy(out=qs2[:, 1, :], in_=qs2[:, 0, :])
        kt_f = keep.tile([P, 8], F32, name="kt_f")
        nc.vector.tensor_copy(out=kt_f[:], in_=kt_b[:].rearrange("p c j -> p (c j)"))
        qt2 = keep.tile([P, T], F32, name="qt2")
        nc.vector.tensor_scalar(out=qt2[:], in0=qt_b[:], scalar1=2.0, scalar2=None, op0=ALU.mult)
        g_f = keep.tile([P, 8], F32, name="g_f")
        nc.vector.tensor_copy(out=g_f[:], in_=g_b[:].rearrange("p c j -> p (c j)"))

        k_codes = keep.tile([P, C, 512], U32, name="k_codes", align_bytes=64)
        k_scales = keep.tile([P, C, 512], U8, name="k_scales", align_bytes=64)
        v_codes = keep.tile([P, C, 512], U32, name="v_codes", align_bytes=64)
        v_scales = keep.tile([P, C, 512], U8, name="v_scales", align_bytes=64)
        q_codes = keep.tile([P, T, P], U32, name="q_codes", align_bytes=64)
        q_scales = keep.tile([P, T, P], U8, name="q_scales", align_bytes=64)
        kt_row = keep.tile([P, C, 512], BF16, name="kt_row")
        vt_row = keep.tile([P, C, 512], F32, name="vt_row")
        ss = keep.tile([P, 8], F32, name="ss")
        vt16 = keep.tile([P, 8], F32, name="vt16")
        g_row = psum.tile([P, C, 512], BF16, name="g_row", tag="g_row")
        ymin = keep.tile([P, T], F32, name="ymin")
        rsum = keep.tile([P, T], F32, name="rsum")
        rinv = keep.tile([P, T], F32, name="rinv")
        ut = keep.tile([P, T], F32, name="ut")
        us2 = keep.tile([P, T], F32, name="us2")
        sm = keep.tile([P, 3, T], F32, name="sm")

        def row_of(cols, c, tag, bufs, out, copy):
            ps = psum.tile([P, 2, 2, P], F32, name="row_ps", tag=tag, bufs=bufs)
            for u in range(2):
                for e in range(2):
                    n = 4 * c + 2 * u + e
                    nc.tensor.transpose(ps[:, u, e, :], cols[:, n : n + 1].to_broadcast([P, P]), ident[:])
            copy(
                out=out[:, c, :].rearrange("p (u m e) -> p u m e", u=2, e=2),
                in_=ps[:].rearrange("p u e m -> p u m e"),
            )

        def g_order():
            for c in range(C):
                for u in range(2):
                    for e in range(2):
                        nc.tensor.matmul(
                            g_row[:, c, 256 * u : 256 * u + 256],
                            lhsT=g_b[:, c, 2 * u + e : 2 * u + e + 1].to_broadcast([P, P]),
                            rhs=spread[:, e, :, :].rearrange("p m e -> p (m e)"),
                            start=(e == 0),
                            stop=(e == 1),
                        )

        qf = {}
        qT = {}
        kT = {}
        kg = {}
        qg = {}

        def q_product(pair):
            qf[pair] = work.tile([P, 2, D], BF16, name="qf", tag="qf", bufs=5)
            nc.vector.tensor_tensor(
                out=qf[pair][:].rearrange("p i d -> p (i d)"),
                in0=q_raw[:, 2 * pair : 2 * pair + 2, :].rearrange("p i d -> p (i d)").bitcast(FP8),
                in1=qs2[:].rearrange("p i d -> p (i d)"),
                op=ALU.mult,
            )

        def q_transpose(pair):
            qT[pair] = psum.tile([P, 2, 2, P], F32, name="qT", tag="qT")
            for i2 in range(2):
                words = qf[pair][:, i2, :].bitcast(F32)
                for u in range(2):
                    nc.tensor.transpose(qT[pair][:, i2, u, :], words[:, u : 256 : 2], ident[:])

        def q_interleave(pair):
            if pair % 2 == 0:
                qg[pair // 2] = work.tile([P, 2, 2 * P * 4], BF16, name="qg", tag="qg", align_bytes=64)
            nc.scalar.copy(
                out=qg[pair // 2][:, pair % 2, :].bitcast(F32).rearrange("p (i n u) -> p i n u", i=2, u=2),
                in_=qT[pair][:].rearrange("p i u n -> p i n u"),
            )

        def q_quantize(pair, pairs):
            tiles = slice(2 * pair, 2 * (pair + pairs))
            nc.vector.quantize_mx(
                out=q_codes[:, tiles, :].rearrange("p i n -> p (i n)").bitcast(FP8X4),
                scales=q_scales[:, tiles, :].rearrange("p i n -> p (i n)"),
                in_=qg[pair // 2][:, pair % 2 : pair % 2 + pairs, :].rearrange("p a b -> p (a b)"),
            )

        def k_transpose(c, u, tag, bufs):
            kT[c, u] = psum.tile([P, 2, 2, P], F32, name="kT", tag=tag, bufs=bufs)
            for e in range(2):
                words = k_raw[:, c, 2 * u + e, :].bitcast(F32)
                for w in range(2):
                    nc.tensor.transpose(kT[c, u][:, e, w, :], words[:, w : 256 : 2], ident[:])

        def k_interleave(c, u, copy):
            if u == 0:
                kg[c] = work.tile([P, 2048], BF16, name="kg", tag="kg", align_bytes=64)
            copy(
                out=kg[c][:, 1024 * u : 1024 * u + 1024].bitcast(F32).rearrange("p (m e w) -> p m e w", e=2, w=2),
                in_=kT[c, u][:].rearrange("p e w m -> p m e w"),
            )

        def k_quantize(c):
            nc.vector.quantize_mx(out=k_codes[:, c, :].bitcast(FP8X4), scales=k_scales[:, c, :], in_=kg[c][:])

        vg = {}

        def value_squares(c):
            for j in range(4):
                n = 4 * c + j
                junk_v = work.tile([P, E], BF16, name="junk_v", tag="junk_s", bufs=2)
                nc.scalar.activation(
                    junk_v[:], v_raw[:, c, j, :], ACT.Square, scale=g_f[:, n : n + 1], accum_out=ss[:, n : n + 1]
                )

        def value_times():
            vz = keep.tile([P, 8], F32, name="vz")
            nc.gpsimd.tensor_scalar(
                out=vz[:], in0=ss[:], scalar1=1.0 / 256.0, scalar2=1.0, op0=ALU.mult, op1=ALU.add
            )
            nc.gpsimd.tensor_tensor(out=vt16[:], in0=vz[:], in1=half[:], op=ALU.pow)

        def value_rows():
            for c in range(C):
                row_of(vt16, c, "us", 3, vt_row, nc.scalar.copy)

        def v_interleave(c):
            vg[c] = work.tile([P, E, 4], BF16, name="vg", tag="vg", align_bytes=64)
            for h in range(4):
                cols = slice(128 * h, 128 * h + 128)
                nc.gpsimd.tensor_scalar(
                    out=vg[c][:, cols, :],
                    in0=v_raw[:, c, :, cols].rearrange("p j e -> p e j"),
                    scalar1=1.0,
                    scalar2=0.0,
                    op0=ALU.mult,
                    op1=ALU.add,
                )

        def v_quantize(c):
            nc.vector.quantize_mx(
                out=v_codes[:, c, :].bitcast(FP8X4),
                scales=v_scales[:, c, :],
                in_=vg[c][:].rearrange("p e j -> p (e j)"),
            )

        S, y, ex, w, pg, pT, pgT, pcodes, pscales, us = {}, {}, {}, {}, {}, {}, {}, {}, {}, {}

        def scores_part(i, c):
            if (i, c) not in S:
                S[i, c] = psum.tile([P, 512], F32, name="S", tag="S%d" % c)
            nc.tensor.matmul_mx(
                out=S[i, c][:],
                lhsT=q_codes[:, i, :].bitcast(FP8X4),
                lhsT_scale=q_scales[:, i, :],
                rhs=k_codes[:, c, :].bitcast(FP8X4),
                rhs_scale=k_scales[:, c, :],
                start=True,
                stop=True,
            )

        def scores(i):
            for c in range(C):
                scores_part(i, c)

        def distance_part(i, c):
                if c == 0:
                    y[i] = work.tile([P, C, 512], F32, name="y", tag="y")
                nc.vector.scalar_tensor_tensor(
                    out=y[i][:, c, :],
                    in0=kt_row[:, c, :],
                    scalar=qt2[:, i : i + 1],
                    in1=S[i, c][:],
                    op0=ALU.mult,
                    op1=ALU.subtract,
                )

        def distance(i):
            for c in range(C):
                distance_part(i, c)

        def minimum(i):
            nc.vector.tensor_reduce(
                out=ymin[:, i : i + 1], in_=y[i][:].rearrange("p c m -> p (c m)"), axis=AX.X, op=ALU.min
            )

        def exponent(i):
            ex[i] = work.tile([P, C, 512], F32, name="ex", tag="ex", bufs=6)
            nc.scalar.activation(
                ex[i][:].rearrange("p c m -> p (c m)"),
                y[i][:].rearrange("p c m -> p (c m)"),
                ACT.Exp,
                bias=ymin[:, i : i + 1],
                scale=-1.0,
                accum_out=rsum[:, i : i + 1],
            )

        def inverse(i):
            nc.vector.reciprocal(out=rinv[:, i : i + 1], in_=rsum[:, i : i + 1])

        def weights(i):
            pg[i] = work.tile([P, C, 512], BF16, name="pg", tag="pg")
            nc.vector.scalar_tensor_tensor(
                out=pg[i][:].rearrange("p c m -> p (c m)"),
                in0=ex[i][:].rearrange("p c m -> p (c m)"),
                scalar=rinv[:, i : i + 1],
                in1=g_row[:].rearrange("p c m -> p (c m)"),
                op0=ALU.mult,
                op1=ALU.mult,
            )

        def time_product(i):
            w[i] = work.tile([P, C, 512], F32, name="w", tag="w", bufs=4)
            nc.gpsimd.tensor_tensor(out=w[i][:], in0=ex[i][:], in1=vt_row[:], op=ALU.mult)

        def time_vector(i):
            junk = work.tile([P, C, 512], BF16, name="junk_w", tag="junk_w", bufs=2)
            nc.vector.scalar_tensor_tensor(
                out=junk[:].rearrange("p c m -> p (c m)"),
                in0=ex[i][:].rearrange("p c m -> p (c m)"),
                scalar=rinv[:, i : i + 1],
                in1=vt_row[:].rearrange("p c m -> p (c m)"),
                op0=ALU.mult,
                op1=ALU.mult,
                accum_out=ut[:, i : i + 1],
            )

        def time_sum(i):
            junk = work.tile([P, C, 512], BF16, name="junk_t", tag="junk_w", bufs=2)
            nc.scalar.activation(
                junk[:].rearrange("p c m -> p (c m)"),
                w[i][:].rearrange("p c m -> p (c m)"),
                ACT.Copy,
                scale=rinv[:, i : i + 1],
                accum_out=ut[:, i : i + 1],
            )

        def pg_transpose(i, tag="pT"):
            pT[i] = psum.tile([P, C, 2, P], F32, name="pT", tag=tag)
            words = pg[i][:].rearrange("p c m -> p (c m)").bitcast(F32)
            for c in range(C):
                for u in range(2):
                    b = 256 * c + 128 * u
                    nc.tensor.transpose(pT[i][:, c, u, :], words[:, b : b + 128], ident[:])

        def pg_interleave(i):
            if i % 2 == 0:
                pgT[i // 2] = work.tile([P, 2, C * P * 4], BF16, name="pgT", tag="pgT", align_bytes=64)
            nc.scalar.copy(
                out=pgT[i // 2][:, i % 2, :].bitcast(F32).rearrange("p (c n u) -> p c n u", c=C, u=2),
                in_=pT[i][:].rearrange("p c u n -> p c n u"),
            )

        def pg_quantize(i, tiles):
            if i % 2 == 0:
                pcodes[i // 2] = work.tile([P, 2, C, P], U32, name="pcodes", tag="pcodes", align_bytes=64)
                pscales[i // 2] = work.tile([P, 2, C, P], U8, name="pscales", tag="pscales", align_bytes=64)
            part = slice(i % 2, i % 2 + tiles)
            nc.vector.quantize_mx(
                out=pcodes[i // 2][:, part, :, :].rearrange("p i c n -> p (i c n)").bitcast(FP8X4),
                scales=pscales[i // 2][:, part, :, :].rearrange("p i c n -> p (i c n)"),
                in_=pgT[i // 2][:, part, :].rearrange("p i x -> p (i x)"),
            )

        def aggregate(i, tag="us", bufs=3):
            us[i] = psum.tile([P, E], F32, name="us", tag=tag, bufs=bufs)
            aggregate_again(i)

        def aggregate_again(i):
            for c in range(C):
                nc.tensor.matmul_mx(
                    out=us[i][:],
                    lhsT=pcodes[i // 2][:, i % 2, c, :].bitcast(FP8X4),
                    lhsT_scale=pscales[i // 2][:, i % 2, c, :],
                    rhs=v_codes[:, c, :].bitcast(FP8X4),
                    rhs_scale=v_scales[:, c, :],
                    start=(c == 0),
                    stop=(c == C - 1),
                )

        def square_sum(i):
            junk = work.tile([P, E], BF16, name="junk_s", tag="junk_s", bufs=2)
            nc.scalar.activation(junk[:], us[i][:], ACT.Square, scale=1.0 / 16.0, accum_out=us2[:, i : i + 1])

        def root_square(i, tiles=2):
            cols = slice(i, i + tiles)
            nc.gpsimd.tensor_tensor(out=sm[:, 0, cols], in0=ut[:, cols], in1=ut[:, cols], op=ALU.mult)

        def root(i, tiles=2):
            cols = slice(i, i + tiles)
            nc.gpsimd.tensor_tensor(out=sm[:, 1, cols], in0=sm[:, 0, cols], in1=us2[:, cols], op=ALU.subtract)
            nc.gpsimd.tensor_tensor(out=sm[:, 2, cols], in0=sm[:, 1, cols], in1=nhalf[:, 0:tiles], op=ALU.pow)

        out_view = out.rearrange("(p i) e -> p i e", i=T)

        def finish(i, on_vector=False):
            o = work.tile([P, E], F32, name="o", tag="o", bufs=6)
            if on_vector:
                nc.vector.tensor_scalar(out=o[:], in0=us[i][:], scalar1=sm[:, 2, i : i + 1], scalar2=None, op0=ALU.mult)
            else:
                nc.scalar.activation(o[:], us[i][:], ACT.Copy, scale=sm[:, 2, i : i + 1])
            nc.sync.dma_start(out=out_view[:, i, :], in_=o[:])

        k_transpose(0, 0, "us", 3)
        k_interleave(0, 0, nc.scalar.copy)
        q_product(0)
        k_transpose(0, 1, "us", 3)
        k_interleave(0, 1, nc.scalar.copy)
        q_transpose(0)
        q_interleave(0)
        k_transpose(1, 0, "pT", None)
        k_interleave(1, 0, nc.scalar.copy)
        q_product(1)
        k_transpose(1, 1, "us", 3)
        k_interleave(1, 1, nc.scalar.copy)
        for c in range(C):
            row_of(kt_f, c, "S%d" % c, None, kt_row, nc.scalar.copy)
        q_product(2)
        k_quantize(0)
        q_quantize(0, 1)
        scores_part(0, 0)
        q_transpose(1)
        q_interleave(1)
        q_product(3)
        distance_part(0, 0)
        k_quantize(1)
        scores_part(0, 1)
        q_quantize(1, 1)
        q_product(4)
        value_squares(0)
        q_transpose(2)
        q_interleave(2)
        value_squares(1)
        for c in range(C):
            v_interleave(c)
        value_times()

        for i in range(T):
            last = i == T - 1
            if i >= 2:
                inverse(i - 2)
            if i == 0:
                distance_part(0, 1)
            else:
                distance(i)
            if not last:
                scores(i + 1)
                if i >= 1:
                    scores_part(i + 1, 1)
            else:
                aggregate(i - 4, "S0", None)
            if i == 0:
                q_transpose(3)
                g_order()
            if i >= 3:
                pg_interleave(i - 3)
                time_sum(i - 3)
            if i >= 5:
                square_sum(i - 5)
            if i >= 6 and i % 2 == 0:
                root(i - 6)
            if i >= 7 and i % 2 == 1 and not last:
                finish(i - 7)
                finish(i - 6)
            for p in range(4, 8):
                if i == Q_STEP[p] + 1:
                    q_interleave(p)
            for p in range(4, 8):
                if i == Q_STEP[p]:
                    q_transpose(p)
            if i >= 2:
                weights(i - 2)
                pg_transpose(i - 2)
            if i >= 4 and i % 2 == 0:
                root_square(i - 4)
            if last:
                inverse(T - 2)
            minimum(i)
            exponent(i)
            if i == 0:
                q_interleave(3)
            if i == 1:
                value_rows()
                time_product(0)
                time_product(1)
            if 2 <= i < T - 2:
                if i not in UT_V:
                    time_product(i)
            for p in range(5, 8):
                if i == QP_STEP[p]:
                    q_product(p)
            for p in (2, 4, 6):
                if i == QQ_STEP[p]:
                    q_quantize(p, 2)
            if i in (2, 3):
                v_quantize(i - 2)
            if i >= 4 and i % 2 == 0:
                pg_quantize(i - 4, 2)
                aggregate(i - 4)
            if i >= 5 and i % 2 == 1 and not last:
                aggregate(i - 4)

        weights(T - 2)
        pg_transpose(T - 2, "qT")
        pg_quantize(T - 4, 1)
        aggregate(T - 4, "S1", None)
        pg_interleave(T - 3)
        time_vector(T - 3)
        pg_interleave(T - 2)
        finish(T - 8)
        finish(T - 7)
        inverse(T - 1)
        root_square(T - 4)
        weights(T - 1)
        pg_transpose(T - 1)
        pg_quantize(T - 3, 1)
        aggregate(T - 3)
        pg_quantize(T - 2, 1)
        aggregate(T - 2)
        square_sum(T - 5)
        root(T - 6)
        pg_interleave(T - 1)
        time_vector(T - 2)
        pg_quantize(T - 1, 1)
        aggregate(T - 1, "qT", None)
        time_vector(T - 1)
        square_sum(T - 4)
        square_sum(T - 3)
        root(T - 4)
        root_square(T - 2)
        finish(T - 6, on_vector=True)
        square_sum(T - 2)
        square_sum(T - 1)
        root(T - 2)
        finish(T - 5, on_vector=True)
        finish(T - 4)
        finish(T - 3, on_vector=True)
        finish(T - 2)
        finish(T - 1, on_vector=True)
